import numpy as np
import ml_dtypes


def mxq(x, axis, fmt="e4m3"):
    dtype, down = {"e4m3": (ml_dtypes.float8_e4m3fn, 7), "e5m2": (ml_dtypes.float8_e5m2, 14)}[fmt]
    v = np.moveaxis(np.asarray(x, np.float32).astype(ml_dtypes.bfloat16).astype(np.float64), axis, -1)
    blocks = v.reshape(v.shape[:-1] + (-1, 32))
    amax = np.abs(blocks).max(-1, keepdims=True)
    byte = np.maximum(np.where(amax > 0, np.frexp(amax)[1] - 1 + 127, 0) - down, 1)
    scale = np.exp2(byte - 127.0)
    codes = (blocks / scale).astype(np.float32).astype(dtype).astype(np.float64)
    return np.moveaxis((codes * scale).reshape(v.shape), -1, axis)


WIDE = False


def mx_kscale(k):
    if not WIDE:
        return np.ones(k)
    levels = np.array([10, -10, 5, -5, 0])
    if k % 512:
        return np.exp2(np.random.permutation(np.resize(levels, k // 32))).repeat(32)
    a = np.empty((k // 512, 16))
    for p in range(k // 512):
        a[p, :8] = np.random.permutation(np.resize(levels, 8))
        for g in range(8):
            far = levels[np.abs(levels - a[p, g]) >= 10]
            a[p, g + 8] = far[np.random.randint(len(far))]
    return np.exp2(a.ravel()).repeat(32)


def f64(x):
    return np.asarray(x).astype(np.float64)


def striped(idx):
    return np.tile(idx.reshape(-1, 16).T, (8, 1)).astype(np.uint16)


def unstriped(offs):
    return offs[:16].T.reshape(-1).astype(np.int64)


def striped8(idx):
    return np.concatenate([x.reshape(-1, 16).T for x in idx]).astype(np.uint16)


def runs(offs, k):
    lists = np.stack([offs[16 * r : 16 * r + 16].T.reshape(-1) for r in range(8)]).astype(np.int64)
    return lists[np.arange(k) % 512 // 64]


def pack_weight(w):
    k, n = w.shape
    w = f64(np.asarray(w, np.float32).astype(ml_dtypes.bfloat16)).reshape(k // 32, 32, n)
    amax = np.abs(w).max(1)
    byte = np.clip(np.where(amax > 0, np.frexp(amax)[1] - 1 + 127 - 7, 1), 1, 254)
    scaled = (w * np.exp2(127.0 - byte)[:, None, :]).reshape(k, n).astype(np.float32)
    words = np.ascontiguousarray(scaled.reshape(k // 512, 128, 4, n).transpose(0, 1, 3, 2)).astype(ml_dtypes.float8_e4m3fn).view(np.uint8)
    return words, np.ascontiguousarray(byte.astype(np.uint8).reshape(k // 512, 16, n))


def unpack_weight(words, scales):
    g, p, n, _ = words.shape
    vals = np.ascontiguousarray(words).view(ml_dtypes.float8_e4m3fn).astype(np.float64) * np.repeat(np.exp2(scales.astype(np.float64) - 127.0), 8, axis=1)[..., None]
    return vals.transpose(0, 1, 3, 2).reshape(g * 512, n)


K, T, S, N, H = 1024, 2048, 512, 512, 512


def setup_inputs():
    n = np.random.standard_normal
    s = mx_kscale(K)[:, None]
    u = mx_kscale(H)
    packed_xT = pack_weight(n((K, T)) * s)
    return {
        "x_words": packed_xT[0],
        "x_scales": packed_xT[1],
        "w1": (n((K, H)) / np.sqrt(K) / s).astype(np.float32),
        "gn": (np.random.uniform(0.5, 1.5, (H, 1)) * u[:, None]).astype(np.float32),
        "w2": (n((H, N)) / np.sqrt(H) / u[:, None]).astype(np.float32),
        "offs": striped(np.random.permutation(T)[:S]),
        "p1": striped8(np.stack([np.random.permutation(S) for _ in range(8)])),
        "p2": striped8(np.stack([np.random.permutation(S) for _ in range(8)])),
    }


def reference(x_words, x_scales, w1, gn, w2, offs, p1, p2):
    xq = unpack_weight(x_words, x_scales)[:, unstriped(offs)]
    y = mxq(f64(w1), 0, "e4m3").T @ xq
    q = (y) ** 2
    z = f64(gn) * (y / (np.sqrt(0.5 * (q + q[np.arange(H)[:, None], runs(p1, H)] + q[np.arange(H)[:, None], runs(p2, H)]) + 1)))
    return mxq(f64(w2), 0, "e4m3").T @ mxq(z, 0, "e4m3")

@@ -1,0 +1,211 @@
+from contextlib import ExitStack
+
+import concourse.mybir as mybir
+
+K, T, S, N, H = 1024, 2048, 512, 512, 512
+FLOPS = 2 * K * H * S + 2 * H * N * S
+
+F32 = mybir.dt.float32
+BF16 = mybir.dt.bfloat16
+I32 = mybir.dt.int32
+U32 = mybir.dt.uint32
+U16 = mybir.dt.uint16
+U8 = mybir.dt.uint8
+FP8X4 = mybir.dt.float8_e4m3fn_x4
+ACT = mybir.ActivationFunctionType
+ALU = mybir.AluOpType
+
+P = 128
+PACK = 4
+K_PASS = P * PACK
+PASSES = K // K_PASS
+CHUNKS = (256, 128, 128)
+SCALAR_ROWS = 48
+
+
+def tile_picked_lrn8_none_p_kernel(tc, x_words, x_scales, w1, gn, w2, offs, p1, p2, out):
+    nc = tc.nc
+    with ExitStack() as ctx:
+        held = ctx.enter_context(tc.tile_pool(name="held", bufs=1))
+        psum = ctx.enter_context(tc.psum_pool(name="psum", bufs=1))
+
+        picked = held.tile([P, S // 16], U16, name="picked")
+        places = [held.tile([P, S // 16], U16, name="places%d" % a) for a in range(2)]
+        scale_table = held.tile([P, T], U8, name="scale_table")
+        nc.vector.memset(scale_table[:].bitcast(I32), 0)
+
+        for quad in range(4):
+            nc.scalar.dma_start(
+                scale_table[32 * quad : 32 * quad + 4 * PASSES, :].bitcast(I32),
+                x_scales[:, 4 * quad : 4 * quad + 4, :].bitcast(I32),
+            )
+
+        warm = held.tile([P, 1], F32, name="warm")
+        nc.vector.memset(warm[:], 1.0)
+        warm_out = held.tile([P, 1], F32, name="warm_out")
+        nc.scalar.activation(out=warm_out[:], in_=warm[:], func=ACT.Abs_reciprocal_sqrt)
+
+        w1_raw = [held.tile([P, PACK, H], F32, name="w1_raw%d" % g) for g in range(PASSES)]
+        nc.sync.dma_start(w1_raw[0][:], w1[0:K_PASS, :].rearrange("(p j) c -> p j c", j=PACK))
+        nc.sync.dma_start(picked[:], offs)
+        nc.sync.dma_start(places[0][:], p1)
+        nc.sync.dma_start(places[1][:], p2)
+        gain = held.tile([P, PACK], F32, name="gain")
+        nc.sync.dma_start(gain[:], gn.rearrange("(p t) o -> p (t o)", t=PACK))
+        nc.sync.dma_start(w1_raw[1][:], w1[K_PASS : 2 * K_PASS, :].rearrange("(p j) c -> p j c", j=PACK))
+        word_table = [held.tile([P, T], I32, name="word_table%d" % g) for g in range(PASSES)]
+        for g in range(PASSES):
+            nc.sync.dma_start(word_table[g][:], x_words[g].rearrange("p n t -> p (n t)").bitcast(I32))
+        w2_raw = held.tile([P, PACK, N], F32, name="w2_raw")
+        nc.sync.dma_start(w2_raw[:], w2.rearrange("(p j) c -> p j c", j=PACK))
+
+        w1_codes, w1_scales = [], []
+        for g in range(PASSES):
+            grouped = held.tile([P, H * PACK], BF16, name="w1_grouped%d" % g, align_bytes=64)
+            dst = grouped[:].rearrange("p (t m j) -> p m j t", t=PACK, j=PACK)
+            src = w1_raw[g][:].rearrange("p j (m t) -> p m j t", t=PACK)
+            nc.scalar.copy(out=dst[:, 0:SCALAR_ROWS], in_=src[:, 0:SCALAR_ROWS])
+            nc.vector.tensor_copy(out=dst[:, SCALAR_ROWS:P], in_=src[:, SCALAR_ROWS:P])
+            codes = held.tile([P, H], U32, name="w1_codes%d" % g, tag="w1_codes%d" % g, align_bytes=64)
+            scales = held.tile([P, H], U8, name="w1_scales%d" % g, align_bytes=64)
+            nc.vector.quantize_mx(out=codes[:].bitcast(FP8X4), scales=scales[:], in_=grouped[:])
+            w1_codes.append(codes)
+            w1_scales.append(scales)
+            if g == 0:
+                x_scale = held.tile([P, S], U8, name="x_scale", align_bytes=64)
+                nc.vector.tensor_copy(x_scale[:], scale_table[:].indirect(picked[:]))
+
+        y = [psum.tile([P, S], F32, name="y%d" % t, tag="y%d" % t) for t in range(PACK)]
+        for g in range(PASSES):
+            x_codes = held.tile([P, S], U32, name="x_codes%d" % g, align_bytes=64)
+            nc.vector.tensor_copy(x_codes[:], word_table[g][:].bitcast(U32).indirect(picked[:]))
+            for t in range(PACK):
+                cols = slice(P * t, P * (t + 1))
+                nc.tensor.matmul_mx(
+                    out=y[t][:],
+                    lhsT=w1_codes[g][:, cols].bitcast(FP8X4),
+                    lhsT_scale=w1_scales[g][:, cols],
+                    rhs=x_codes[:].bitcast(FP8X4),
+                    rhs_scale=x_scale[4 * g : P, :],
+                    start=(g == 0),
+                    stop=(g == PASSES - 1),
+                )
+
+        starts = [sum(CHUNKS[:c]) for c in range(len(CHUNKS))]
+        squares = [held.tile([P, S], F32, name="squares%d" % t) for t in range(PACK)]
+        own = [held.tile([P, PACK, n], F32, name="own%d" % c) for c, n in enumerate(CHUNKS)]
+        gained = [held.tile([P, PACK, n], F32, name="gained%d" % c) for c, n in enumerate(CHUNKS)]
+
+        def read_y(c, t):
+            toks = slice(starts[c], starts[c] + CHUNKS[c])
+            nc.scalar.activation(out=own[c][:, t, :], in_=y[t][:, toks], func=ACT.Square)
+
+        def gain_y(c, t):
+            toks = slice(starts[c], starts[c] + CHUNKS[c])
+            nc.scalar.activation(out=gained[c][:, t, :], in_=y[t][:, toks], func=ACT.Copy, scale=gain[:, t : t + 1])
+
+        for t in range(PACK):
+            nc.scalar.activation(out=squares[t][:], in_=y[t][:], func=ACT.Square)
+            read_y(0, t)
+        for t in range(PACK):
+            read_y(1, t)
+
+        w2_grouped = held.tile([P, N * PACK], BF16, name="w2_grouped", tag="w1_codes1", align_bytes=64)
+        w2_codes = held.tile([P, N], U32, name="w2_codes", align_bytes=64)
+        w2_scales = held.tile([P, N], U8, name="w2_scales", align_bytes=64)
+
+        roots = [held.tile([P, PACK, n], F32, name="roots%d" % c) for c, n in enumerate(CHUNKS)]
+
+        sums = [held.tile([P, PACK, n], F32, name="sums%d" % c) for c, n in enumerate(CHUNKS)]
+
+        def root(c):
+            for t in range(PACK):
+                nc.scalar.activation(
+                    out=roots[c][:, t, :], in_=sums[c][:, t, :], func=ACT.Abs_reciprocal_sqrt, scale=0.5, bias=1.0
+                )
+
+        def neighbours(c):
+            n = CHUNKS[c]
+            cols = slice(starts[c] // 16, (starts[c] + n) // 16)
+            two = held.tile([P, PACK, n], F32, name="two%d" % c)
+            three = sums[c]
+
+            def first(t):
+                nc.vector.tensor_tensor(two[:, t, :], squares[t][:].indirect(places[0][:, cols]), own[c][:, t, :], ALU.add)
+
+            def second(t):
+                nc.vector.tensor_tensor(three[:, t, :], squares[t][:].indirect(places[1][:, cols]), two[:, t, :], ALU.add)
+
+            first(0)
+            for t in range(1, PACK):
+                first(t)
+                second(t - 1)
+            second(PACK - 1)
+
+        def finish(c):
+            n = CHUNKS[c]
+            z = held.tile([P, n * PACK], BF16, name="z%d" % c, align_bytes=64)
+            nc.vector.tensor_tensor(
+                z[:].rearrange("p (c i t) -> p c t i", i=4, t=PACK),
+                gained[c][:].rearrange("p t (c i) -> p c t i", i=4),
+                roots[c][:].rearrange("p t (c i) -> p c t i", i=4),
+                ALU.mult,
+            )
+            z_codes = held.tile([P, n], U32, name="z_codes%d" % c, align_bytes=64)
+            z_scales = held.tile([P, n], U8, name="z_scales%d" % c, align_bytes=64)
+            nc.vector.quantize_mx(out=z_codes[:].bitcast(FP8X4), scales=z_scales[:], in_=z[:])
+            banks = 1 if c == 1 else 2
+            per_bank = N // P // banks
+            accs = []
+            for b in range(banks):
+                acc = psum.tile([P, per_bank, n], F32, name="acc%d_%d" % (c, b), tag=("y0" if c == 1 else "acc%d_%d" % (c, b)))
+                for i in range(per_bank):
+                    cols = slice(P * (b * per_bank + i), P * (b * per_bank + i + 1))
+                    nc.tensor.matmul_mx(
+                        out=acc[:, i, :],
+                        lhsT=w2_codes[:, cols].bitcast(FP8X4),
+                        lhsT_scale=w2_scales[:, cols],
+                        rhs=z_codes[:].bitcast(FP8X4),
+                        rhs_scale=z_scales[:],
+                        start=True,
+                        stop=True,
+                    )
+                accs.append(acc)
+            return accs
+
+        def store(c, accs):
+            n = CHUNKS[c]
+            per_bank = N // P // len(accs)
+            for b, acc in enumerate(accs):
+                res = held.tile([P, per_bank, n], F32, name="res%d_%d" % (c, b))
+                rows = out[P * per_bank * b : P * per_bank * (b + 1), starts[c] : starts[c] + n]
+                if c == len(CHUNKS) - 1 and b == 1:
+                    nc.vector.tensor_copy(out=res[:], in_=acc[:])
+                else:
+                    nc.scalar.copy(out=res[:], in_=acc[:])
+                nc.sync.dma_start(rows.rearrange("(i p) n -> p i n", p=P), res[:])
+
+        neighbours(0)
+        neighbours(1)
+        nc.scalar.copy(
+            out=w2_grouped[:].rearrange("p (c i j) -> p c j i", i=4, j=PACK),
+            in_=w2_raw[:].rearrange("p j (c i) -> p c j i", i=4),
+        )
+        nc.vector.quantize_mx(out=w2_codes[:].bitcast(FP8X4), scales=w2_scales[:], in_=w2_grouped[:])
+        for t in range(PACK):
+            gain_y(0, t)
+        root(0)
+        accs0 = finish(0)
+        for t in range(PACK):
+            read_y(2, t)
+        neighbours(2)
+        for c in range(1, len(CHUNKS)):
+            for t in range(PACK):
+                gain_y(c, t)
+        root(1)
+        store(0, accs0)
+        accs1 = finish(1)
+        root(2)
+        accs2 = finish(2)
+        store(1, accs1)
+        store(2, accs2)

@@ -32,13 +32,8 @@ def tile_picked_lrn8_none_p_kernel(tc, x_words, x_scales, w1, gn, w2, offs, p1, 
         picked = held.tile([P, S // 16], U16, name="picked")
         places = [held.tile([P, S // 16], U16, name="places%d" % a) for a in range(2)]
         scale_table = held.tile([P, T], U8, name="scale_table")
-        nc.vector.memset(scale_table[:].bitcast(I32), 0)
+        nc.gpsimd.memset(scale_table[:].bitcast(I32), 0)
 
-        for quad in range(4):
-            nc.scalar.dma_start(
-                scale_table[32 * quad : 32 * quad + 4 * PASSES, :].bitcast(I32),
-                x_scales[:, 4 * quad : 4 * quad + 4, :].bitcast(I32),
-            )
 
         warm = held.tile([P, 1], F32, name="warm")
         nc.vector.memset(warm[:], 1.0)
@@ -47,15 +42,20 @@ def tile_picked_lrn8_none_p_kernel(tc, x_words, x_scales, w1, gn, w2, offs, p1, 
 
         w1_raw = [held.tile([P, PACK, H], F32, name="w1_raw%d" % g) for g in range(PASSES)]
         nc.sync.dma_start(w1_raw[0][:], w1[0:K_PASS, :].rearrange("(p j) c -> p j c", j=PACK))
+        for quad in range(4):
+            nc.sync.dma_start(
+                scale_table[32 * quad : 32 * quad + 4 * PASSES, :].bitcast(I32),
+                x_scales[:, 4 * quad : 4 * quad + 4, :].bitcast(I32),
+            )
         nc.sync.dma_start(picked[:], offs)
-        nc.sync.dma_start(places[0][:], p1)
-        nc.sync.dma_start(places[1][:], p2)
-        gain = held.tile([P, PACK], F32, name="gain")
-        nc.sync.dma_start(gain[:], gn.rearrange("(p t) o -> p (t o)", t=PACK))
         nc.sync.dma_start(w1_raw[1][:], w1[K_PASS : 2 * K_PASS, :].rearrange("(p j) c -> p j c", j=PACK))
         word_table = [held.tile([P, T], I32, name="word_table%d" % g) for g in range(PASSES)]
         for g in range(PASSES):
             nc.sync.dma_start(word_table[g][:], x_words[g].rearrange("p n t -> p (n t)").bitcast(I32))
+        nc.sync.dma_start(places[0][:], p1)
+        nc.sync.dma_start(places[1][:], p2)
+        gain = held.tile([P, PACK], F32, name="gain")
+        nc.sync.dma_start(gain[:], gn.rearrange("(p t) o -> p (t o)", t=PACK))
         w2_raw = held.tile([P, PACK, N], F32, name="w2_raw")
         nc.sync.dma_start(w2_raw[:], w2.rearrange("(p j) c -> p j c", j=PACK))
 
@@ -71,42 +71,58 @@ def tile_picked_lrn8_none_p_kernel(tc, x_words, x_scales, w1, gn, w2, offs, p1, 
             nc.vector.quantize_mx(out=codes[:].bitcast(FP8X4), scales=scales[:], in_=grouped[:])
             w1_codes.append(codes)
             w1_scales.append(scales)
-            if g == 0:
-                x_scale = held.tile([P, S], U8, name="x_scale", align_bytes=64)
-                nc.vector.tensor_copy(x_scale[:], scale_table[:].indirect(picked[:]))
+        x_scale = held.tile([P, S], U8, name="x_scale", align_bytes=64)
+        nc.vector.tensor_copy(x_scale[:], scale_table[:].indirect(picked[:]))
 
-        y = [psum.tile([P, S], F32, name="y%d" % t, tag="y%d" % t) for t in range(PACK)]
+        halves = [slice(0, S // 2), slice(S // 2, S)]
+        y = []
+        for t in range(PACK):
+            parts = halves if t == 0 else [slice(0, S)]
+            y.append([(k, psum.tile([P, k.stop - k.start], F32, name="y%d_%d" % (t, k.start), tag="y%d_%d" % (t, k.start))) for k in parts])
+
+        def y_view(t, toks):
+            for k, bank in y[t]:
+                if k.start <= toks.start and toks.stop <= k.stop:
+                    return bank[:, toks.start - k.start : toks.stop - k.start]
+            raise ValueError("tokens across two banks")
+
+        squares = [held.tile([P, S], F32, name="squares%d" % t) for t in range(PACK)]
         for g in range(PASSES):
             x_codes = held.tile([P, S], U32, name="x_codes%d" % g, align_bytes=64)
-            nc.vector.tensor_copy(x_codes[:], word_table[g][:].bitcast(U32).indirect(picked[:]))
+            for k in halves if g == PASSES - 1 else [slice(0, S)]:
+                nc.vector.tensor_copy(
+                    x_codes[:, k], word_table[g][:].bitcast(U32).indirect(picked[:, k.start // 16 : k.stop // 16])
+                )
             for t in range(PACK):
                 cols = slice(P * t, P * (t + 1))
-                nc.tensor.matmul_mx(
-                    out=y[t][:],
-                    lhsT=w1_codes[g][:, cols].bitcast(FP8X4),
-                    lhsT_scale=w1_scales[g][:, cols],
-                    rhs=x_codes[:].bitcast(FP8X4),
-                    rhs_scale=x_scale[4 * g : P, :],
-                    start=(g == 0),
-                    stop=(g == PASSES - 1),
-                )
+                for k, bank in y[t]:
+                    nc.tensor.matmul_mx(
+                        out=bank[:],
+                        lhsT=w1_codes[g][:, cols].bitcast(FP8X4),
+                        lhsT_scale=w1_scales[g][:, cols],
+                        rhs=x_codes[:, k].bitcast(FP8X4),
+                        rhs_scale=x_scale[4 * g : P, k],
+                        start=(g == 0),
+                        stop=(g == PASSES - 1),
+                    )
 
         starts = [sum(CHUNKS[:c]) for c in range(len(CHUNKS))]
-        squares = [held.tile([P, S], F32, name="squares%d" % t) for t in range(PACK)]
         own = [held.tile([P, PACK, n], F32, name="own%d" % c) for c, n in enumerate(CHUNKS)]
         gained = [held.tile([P, PACK, n], F32, name="gained%d" % c) for c, n in enumerate(CHUNKS)]
 
         def read_y(c, t):
             toks = slice(starts[c], starts[c] + CHUNKS[c])
-            nc.scalar.activation(out=own[c][:, t, :], in_=y[t][:, toks], func=ACT.Square)
+            nc.scalar.activation(out=own[c][:, t, :], in_=y_view(t, toks), func=ACT.Square)
 
         def gain_y(c, t):
             toks = slice(starts[c], starts[c] + CHUNKS[c])
-            nc.scalar.activation(out=gained[c][:, t, :], in_=y[t][:, toks], func=ACT.Copy, scale=gain[:, t : t + 1])
+            nc.scalar.activation(out=gained[c][:, t, :], in_=y_view(t, toks), func=ACT.Copy, scale=gain[:, t : t + 1])
 
         for t in range(PACK):
-            nc.scalar.activation(out=squares[t][:], in_=y[t][:], func=ACT.Square)
-            read_y(0, t)
+            for i, (k, bank) in enumerate(y[t]):
+                nc.scalar.activation(out=squares[t][:, k], in_=bank[:], func=ACT.Square)
+                if i == 0:
+                    read_y(0, t)
         for t in range(PACK):
             read_y(1, t)
 
@@ -158,7 +174,7 @@ def tile_picked_lrn8_none_p_kernel(tc, x_words, x_scales, w1, gn, w2, offs, p1, 
             per_bank = N // P // banks
             accs = []
             for b in range(banks):
-                acc = psum.tile([P, per_bank, n], F32, name="acc%d_%d" % (c, b), tag=("y0" if c == 1 else "acc%d_%d" % (c, b)))
+                acc = psum.tile([P, per_bank, n], F32, name="acc%d_%d" % (c, b), tag=("y0_0" if c == 1 else "y0_256" if (c, b) == (2, 1) else "acc%d_%d" % (c, b)))
                 for i in range(per_bank):
                     cols = slice(P * (b * per_bank + i), P * (b * per_bank + i + 1))
                     nc.tensor.matmul_mx(

@@ -19,8 +19,23 @@ P = 128
 PACK = 4
 K_PASS = P * PACK
 PASSES = K // K_PASS
-CHUNKS = (256, 128, 128)
-SCALAR_ROWS = 48
+LIST_COLUMN = 16
+QUADRANT = 32
+SCALE_ROWS = 4
+LINE = 4
+HALVES = (slice(0, S // 2), slice(S // 2, S))
+CHUNKS = (slice(0, 256), slice(256, 384), slice(384, 512))
+SCALAR_GROUPS = 32
+OUT_BANKS = 2
+ROWS_PER_BANK = N // OUT_BANKS
+
+
+def width(tokens):
+    return tokens.stop - tokens.start
+
+
+def list_columns(tokens):
+    return slice(tokens.start // LIST_COLUMN, tokens.stop // LIST_COLUMN)
 
 
 def tile_picked_lrn8_none_p_kernel(tc, x_words, x_scales, w1, gn, w2, offs, p1, p2, out):
@@ -29,29 +44,24 @@ def tile_picked_lrn8_none_p_kernel(tc, x_words, x_scales, w1, gn, w2, offs, p1, 
         held = ctx.enter_context(tc.tile_pool(name="held", bufs=1))
         psum = ctx.enter_context(tc.psum_pool(name="psum", bufs=1))
 
-        picked = held.tile([P, S // 16], U16, name="picked")
-        places = [held.tile([P, S // 16], U16, name="places%d" % a) for a in range(2)]
+        picked = held.tile([P, S // LIST_COLUMN], U16, name="picked")
+        places = [held.tile([P, S // LIST_COLUMN], U16, name="places%d" % a) for a in range(2)]
+
         scale_table = held.tile([P, T], U8, name="scale_table")
         nc.gpsimd.memset(scale_table[:].bitcast(I32), 0)
 
-
-        warm = held.tile([P, 1], F32, name="warm")
-        nc.vector.memset(warm[:], 1.0)
-        warm_out = held.tile([P, 1], F32, name="warm_out")
-        nc.scalar.activation(out=warm_out[:], in_=warm[:], func=ACT.Abs_reciprocal_sqrt)
-
         w1_raw = [held.tile([P, PACK, H], F32, name="w1_raw%d" % g) for g in range(PASSES)]
         nc.sync.dma_start(w1_raw[0][:], w1[0:K_PASS, :].rearrange("(p j) c -> p j c", j=PACK))
-        for quad in range(4):
+        for quad in range(P // QUADRANT):
             nc.sync.dma_start(
-                scale_table[32 * quad : 32 * quad + 4 * PASSES, :].bitcast(I32),
-                x_scales[:, 4 * quad : 4 * quad + 4, :].bitcast(I32),
+                scale_table[QUADRANT * quad : QUADRANT * quad + SCALE_ROWS * PASSES, :].bitcast(I32),
+                x_scales[:, SCALE_ROWS * quad : SCALE_ROWS * (quad + 1), :].bitcast(I32),
             )
         nc.sync.dma_start(picked[:], offs)
         nc.sync.dma_start(w1_raw[1][:], w1[K_PASS : 2 * K_PASS, :].rearrange("(p j) c -> p j c", j=PACK))
         word_table = [held.tile([P, T], I32, name="word_table%d" % g) for g in range(PASSES)]
         for g in range(PASSES):
-            nc.sync.dma_start(word_table[g][:], x_words[g].rearrange("p n t -> p (n t)").bitcast(I32))
+            nc.sync.dma_start(word_table[g][:], x_words[g].rearrange("p n j -> p (n j)").bitcast(I32))
         nc.sync.dma_start(places[0][:], p1)
         nc.sync.dma_start(places[1][:], p2)
         gain = held.tile([P, PACK], F32, name="gain")
@@ -61,78 +71,102 @@ def tile_picked_lrn8_none_p_kernel(tc, x_words, x_scales, w1, gn, w2, offs, p1, 
 
         w1_codes, w1_scales = [], []
         for g in range(PASSES):
-            grouped = held.tile([P, H * PACK], BF16, name="w1_grouped%d" % g, align_bytes=64)
-            dst = grouped[:].rearrange("p (t m j) -> p m j t", t=PACK, j=PACK)
+            w1_grouped = held.tile([P, H * PACK], BF16, name="w1_grouped%d" % g, align_bytes=64)
+            dst = w1_grouped[:].rearrange("p (t m j) -> p m j t", t=PACK, j=PACK)
             src = w1_raw[g][:].rearrange("p j (m t) -> p m j t", t=PACK)
-            nc.scalar.copy(out=dst[:, 0:SCALAR_ROWS], in_=src[:, 0:SCALAR_ROWS])
-            nc.vector.tensor_copy(out=dst[:, SCALAR_ROWS:P], in_=src[:, SCALAR_ROWS:P])
+            nc.scalar.copy(out=dst[:, 0:SCALAR_GROUPS], in_=src[:, 0:SCALAR_GROUPS])
+            nc.vector.tensor_copy(out=dst[:, SCALAR_GROUPS:P], in_=src[:, SCALAR_GROUPS:P])
             codes = held.tile([P, H], U32, name="w1_codes%d" % g, tag="w1_codes%d" % g, align_bytes=64)
             scales = held.tile([P, H], U8, name="w1_scales%d" % g, align_bytes=64)
-            nc.vector.quantize_mx(out=codes[:].bitcast(FP8X4), scales=scales[:], in_=grouped[:])
+            nc.vector.quantize_mx(out=codes[:].bitcast(FP8X4), scales=scales[:], in_=w1_grouped[:])
             w1_codes.append(codes)
             w1_scales.append(scales)
         x_scale = held.tile([P, S], U8, name="x_scale", align_bytes=64)
         nc.vector.tensor_copy(x_scale[:], scale_table[:].indirect(picked[:]))
 
-        halves = [slice(0, S // 2), slice(S // 2, S)]
         y = []
         for t in range(PACK):
-            parts = halves if t == 0 else [slice(0, S)]
-            y.append([(k, psum.tile([P, k.stop - k.start], F32, name="y%d_%d" % (t, k.start), tag="y%d_%d" % (t, k.start))) for k in parts])
+            parts = HALVES if t == 0 else (slice(0, S),)
+            names = ["y%d_%d" % (t, part.start) for part in parts]
+            y.append([(part, psum.tile([P, width(part)], F32, name=nm, tag=nm)) for part, nm in zip(parts, names)])
 
-        def y_view(t, toks):
-            for k, bank in y[t]:
-                if k.start <= toks.start and toks.stop <= k.stop:
-                    return bank[:, toks.start - k.start : toks.stop - k.start]
-            raise ValueError("tokens across two banks")
+        def y_view(t, tokens):
+            part, bank = [entry for entry in y[t] if entry[0].start <= tokens.start < entry[0].stop][0]
+            return bank[:, tokens.start - part.start : tokens.stop - part.start]
 
         squares = [held.tile([P, S], F32, name="squares%d" % t) for t in range(PACK)]
-        for g in range(PASSES):
-            x_codes = held.tile([P, S], U32, name="x_codes%d" % g, align_bytes=64)
-            for k in halves if g == PASSES - 1 else [slice(0, S)]:
-                nc.vector.tensor_copy(
-                    x_codes[:, k], word_table[g][:].bitcast(U32).indirect(picked[:, k.start // 16 : k.stop // 16])
+        x_codes = [held.tile([P, S], U32, name="x_codes%d" % g, align_bytes=64) for g in range(PASSES)]
+
+        def first_layer(t, g, start):
+            cols = slice(P * t, P * (t + 1))
+            for part, bank in y[t]:
+                nc.tensor.matmul_mx(
+                    out=bank[:],
+                    lhsT=w1_codes[g][:, cols].bitcast(FP8X4),
+                    lhsT_scale=w1_scales[g][:, cols],
+                    rhs=x_codes[g][:, part].bitcast(FP8X4),
+                    rhs_scale=x_scale[SCALE_ROWS * g : P, part],
+                    start=start,
+                    stop=not start,
                 )
+
+        for g in range(PASSES):
+            for part in HALVES if g == PASSES - 1 else (slice(0, S),):
+                nc.vector.tensor_copy(
+                    x_codes[g][:, part], word_table[g][:].bitcast(U32).indirect(picked[:, list_columns(part)])
+                )
+            for t in range(PACK - 1):
+                first_layer(t, g, g == 0)
+        first_layer(PACK - 1, 1, True)
+        first_layer(PACK - 1, 0, False)
+
+        last = CHUNKS[-1]
+        own = held.tile([P, PACK, last.start], F32, name="own")
+        own_last = [held.tile([P, width(last)], F32, name="own_last%d" % t) for t in range(PACK)]
+        gained = [held.tile([P, PACK, S // 2], F32, name="gained%d" % h, tag="gained%d" % h) for h in range(2)]
+        for t in range(PACK):
+            for part, bank in y[t]:
+                nc.scalar.activation(out=squares[t][:, part], in_=bank[:], func=ACT.Square)
+                early = slice(part.start, min(part.stop, last.start))
+                nc.scalar.activation(out=own[:, t, early], in_=y_view(t, early), func=ACT.Square)
+            nc.sync.dma_start(own_last[t][:], squares[t][:, last])
+
+        def gain_y(h):
             for t in range(PACK):
-                cols = slice(P * t, P * (t + 1))
-                for k, bank in y[t]:
-                    nc.tensor.matmul_mx(
-                        out=bank[:],
-                        lhsT=w1_codes[g][:, cols].bitcast(FP8X4),
-                        lhsT_scale=w1_scales[g][:, cols],
-                        rhs=x_codes[:, k].bitcast(FP8X4),
-                        rhs_scale=x_scale[4 * g : P, k],
-                        start=(g == 0),
-                        stop=(g == PASSES - 1),
-                    )
-
-        starts = [sum(CHUNKS[:c]) for c in range(len(CHUNKS))]
-        own = [held.tile([P, PACK, n], F32, name="own%d" % c) for c, n in enumerate(CHUNKS)]
-        gained = [held.tile([P, PACK, n], F32, name="gained%d" % c) for c, n in enumerate(CHUNKS)]
-
-        def read_y(c, t):
-            toks = slice(starts[c], starts[c] + CHUNKS[c])
-            nc.scalar.activation(out=own[c][:, t, :], in_=y_view(t, toks), func=ACT.Square)
-
-        def gain_y(c, t):
-            toks = slice(starts[c], starts[c] + CHUNKS[c])
-            nc.scalar.activation(out=gained[c][:, t, :], in_=y_view(t, toks), func=ACT.Copy, scale=gain[:, t : t + 1])
-
-        for t in range(PACK):
-            for i, (k, bank) in enumerate(y[t]):
-                nc.scalar.activation(out=squares[t][:, k], in_=bank[:], func=ACT.Square)
-                if i == 0:
-                    read_y(0, t)
-        for t in range(PACK):
-            read_y(1, t)
+                nc.scalar.activation(
+                    out=gained[h][:, t, :], in_=y_view(t, HALVES[h]), func=ACT.Copy, scale=gain[:, t : t + 1]
+                )
 
         w2_grouped = held.tile([P, N * PACK], BF16, name="w2_grouped", tag="w1_codes1", align_bytes=64)
         w2_codes = held.tile([P, N], U32, name="w2_codes", align_bytes=64)
         w2_scales = held.tile([P, N], U8, name="w2_scales", align_bytes=64)
 
-        roots = [held.tile([P, PACK, n], F32, name="roots%d" % c) for c, n in enumerate(CHUNKS)]
+        def group_w2(half):
+            lines = slice(half * N // (2 * LINE), (half + 1) * N // (2 * LINE))
+            nc.scalar.copy(
+                out=w2_grouped[:].rearrange("p (c i j) -> p c j i", i=LINE, j=PACK)[:, lines],
+                in_=w2_raw[:].rearrange("p j (c i) -> p c j i", i=LINE)[:, lines],
+            )
 
-        sums = [held.tile([P, PACK, n], F32, name="sums%d" % c) for c, n in enumerate(CHUNKS)]
+        def quantise_w2(half):
+            cols = slice(half * N // 2, (half + 1) * N // 2)
+            nc.vector.quantize_mx(
+                out=w2_codes[:, cols].bitcast(FP8X4),
+                scales=w2_scales[:, cols],
+                in_=w2_grouped[:, PACK * cols.start : PACK * cols.stop],
+            )
+
+        roots = [held.tile([P, PACK, width(ch)], F32, name="roots%d" % c) for c, ch in enumerate(CHUNKS)]
+        sums = [held.tile([P, PACK, width(ch)], F32, name="sums%d" % c) for c, ch in enumerate(CHUNKS)]
+
+        def add_first(c, t, partial):
+            mine = own_last[t][:] if CHUNKS[c] == last else own[:, t, CHUNKS[c]]
+            looked_up = squares[t][:].indirect(places[0][:, list_columns(CHUNKS[c])])
+            nc.vector.tensor_tensor(partial[:, t, :], looked_up, mine, ALU.add)
+
+        def add_second(c, t, partial):
+            looked_up = squares[t][:].indirect(places[1][:, list_columns(CHUNKS[c])])
+            nc.vector.tensor_tensor(sums[c][:, t, :], looked_up, partial[:, t, :], ALU.add)
 
         def root(c):
             for t in range(PACK):
@@ -140,45 +174,31 @@ def tile_picked_lrn8_none_p_kernel(tc, x_words, x_scales, w1, gn, w2, offs, p1, 
                     out=roots[c][:, t, :], in_=sums[c][:, t, :], func=ACT.Abs_reciprocal_sqrt, scale=0.5, bias=1.0
                 )
 
-        def neighbours(c):
-            n = CHUNKS[c]
-            cols = slice(starts[c] // 16, (starts[c] + n) // 16)
-            two = held.tile([P, PACK, n], F32, name="two%d" % c)
-            three = sums[c]
+        z = [held.tile([P, width(ch) * PACK], BF16, name="z%d" % c, align_bytes=64) for c, ch in enumerate(CHUNKS)]
 
-            def first(t):
-                nc.vector.tensor_tensor(two[:, t, :], squares[t][:].indirect(places[0][:, cols]), own[c][:, t, :], ALU.add)
-
-            def second(t):
-                nc.vector.tensor_tensor(three[:, t, :], squares[t][:].indirect(places[1][:, cols]), two[:, t, :], ALU.add)
-
-            first(0)
-            for t in range(1, PACK):
-                first(t)
-                second(t - 1)
-            second(PACK - 1)
-
-        def finish(c):
-            n = CHUNKS[c]
-            z = held.tile([P, n * PACK], BF16, name="z%d" % c, align_bytes=64)
+        def normalise(c):
+            h, lo = divmod(CHUNKS[c].start, S // 2)
             nc.vector.tensor_tensor(
-                z[:].rearrange("p (c i t) -> p c t i", i=4, t=PACK),
-                gained[c][:].rearrange("p t (c i) -> p c t i", i=4),
-                roots[c][:].rearrange("p t (c i) -> p c t i", i=4),
+                z[c][:].rearrange("p (u i t) -> p u t i", i=LINE, t=PACK),
+                gained[h][:, :, lo : lo + width(CHUNKS[c])].rearrange("p t (u i) -> p u t i", i=LINE),
+                roots[c][:].rearrange("p t (u i) -> p u t i", i=LINE),
                 ALU.mult,
             )
+
+        out_tags = (("out0", "out1"), ("y0_0", "y1_0"), ("y0_256", "y2_0"))
+
+        def second_layer(c):
+            n = width(CHUNKS[c])
             z_codes = held.tile([P, n], U32, name="z_codes%d" % c, align_bytes=64)
             z_scales = held.tile([P, n], U8, name="z_scales%d" % c, align_bytes=64)
-            nc.vector.quantize_mx(out=z_codes[:].bitcast(FP8X4), scales=z_scales[:], in_=z[:])
-            banks = 1 if c == 1 else 2
-            per_bank = N // P // banks
-            accs = []
-            for b in range(banks):
-                acc = psum.tile([P, per_bank, n], F32, name="acc%d_%d" % (c, b), tag=("y0_0" if c == 1 else "y0_256" if (c, b) == (2, 1) else "acc%d_%d" % (c, b)))
-                for i in range(per_bank):
-                    cols = slice(P * (b * per_bank + i), P * (b * per_bank + i + 1))
+            nc.vector.quantize_mx(out=z_codes[:].bitcast(FP8X4), scales=z_scales[:], in_=z[c][:])
+            banks = []
+            for b in range(OUT_BANKS):
+                bank = psum.tile([P, ROWS_PER_BANK // P, n], F32, name="out%d_%d" % (c, b), tag=out_tags[c][b])
+                for i in range(ROWS_PER_BANK // P):
+                    cols = slice(ROWS_PER_BANK * b + P * i, ROWS_PER_BANK * b + P * (i + 1))
                     nc.tensor.matmul_mx(
-                        out=acc[:, i, :],
+                        out=bank[:, i, :],
                         lhsT=w2_codes[:, cols].bitcast(FP8X4),
                         lhsT_scale=w2_scales[:, cols],
                         rhs=z_codes[:].bitcast(FP8X4),
@@ -186,42 +206,44 @@ def tile_picked_lrn8_none_p_kernel(tc, x_words, x_scales, w1, gn, w2, offs, p1, 
                         start=True,
                         stop=True,
                     )
-                accs.append(acc)
-            return accs
+                banks.append(bank)
+            return banks
 
-        def store(c, accs):
-            n = CHUNKS[c]
-            per_bank = N // P // len(accs)
-            for b, acc in enumerate(accs):
-                res = held.tile([P, per_bank, n], F32, name="res%d_%d" % (c, b))
-                rows = out[P * per_bank * b : P * per_bank * (b + 1), starts[c] : starts[c] + n]
-                if c == len(CHUNKS) - 1 and b == 1:
-                    nc.vector.tensor_copy(out=res[:], in_=acc[:])
-                else:
-                    nc.scalar.copy(out=res[:], in_=acc[:])
-                nc.sync.dma_start(rows.rearrange("(i p) n -> p i n", p=P), res[:])
+        def store(c, banks, copies):
+            for b, (bank, copy) in enumerate(zip(banks, copies)):
+                result = held.tile([P, ROWS_PER_BANK // P, width(CHUNKS[c])], F32, name="result%d_%d" % (c, b))
+                copy(out=result[:], in_=bank[:])
+                rows = out[ROWS_PER_BANK * b : ROWS_PER_BANK * (b + 1), CHUNKS[c]]
+                nc.sync.dma_start(rows.rearrange("(i p) n -> p i n", p=P), result[:])
 
-        neighbours(0)
-        neighbours(1)
-        nc.scalar.copy(
-            out=w2_grouped[:].rearrange("p (c i j) -> p c j i", i=4, j=PACK),
-            in_=w2_raw[:].rearrange("p j (c i) -> p c j i", i=4),
-        )
-        nc.vector.quantize_mx(out=w2_codes[:].bitcast(FP8X4), scales=w2_scales[:], in_=w2_grouped[:])
+        partials = [held.tile([P, PACK, width(CHUNKS[c])], F32, name="partial%d" % c) for c in range(2)]
         for t in range(PACK):
-            gain_y(0, t)
+            for c in range(2):
+                add_first(c, t, partials[c])
+            for c in range(2):
+                add_second(c, t, partials[c])
+        group_w2(0)
+        quantise_w2(0)
+        gain_y(0)
         root(0)
-        accs0 = finish(0)
-        for t in range(PACK):
-            read_y(2, t)
-        neighbours(2)
-        for c in range(1, len(CHUNKS)):
-            for t in range(PACK):
-                gain_y(c, t)
+        group_w2(1)
+        normalise(0)
+        quantise_w2(1)
+        banks0 = second_layer(0)
+
+        partial_last = held.tile([P, PACK, width(last)], F32, name="partial2", tag="gained0")
+        add_first(2, 0, partial_last)
+        for t in range(1, PACK):
+            add_first(2, t, partial_last)
+            add_second(2, t - 1, partial_last)
+        add_second(2, PACK - 1, partial_last)
+        gain_y(1)
+        store(0, banks0, (nc.scalar.copy, nc.scalar.copy))
         root(1)
-        store(0, accs0)
-        accs1 = finish(1)
+        normalise(1)
+        banks1 = second_layer(1)
         root(2)
-        accs2 = finish(2)
-        store(1, accs1)
-        store(2, accs2)
+        normalise(2)
+        banks2 = second_layer(2)
+        store(1, banks1, (nc.scalar.copy, nc.vector.tensor_copy))
+        store(2, banks2, (nc.scalar.copy, nc.vector.tensor_copy))

@@ -25,9 +25,7 @@ SCALE_ROWS = 4
 LINE = 4
 HALVES = (slice(0, S // 2), slice(S // 2, S))
 CHUNKS = (slice(0, 256), slice(256, 384), slice(384, 512))
-SCALAR_GROUPS = 32
-OUT_BANKS = 2
-ROWS_PER_BANK = N // OUT_BANKS
+SCALAR_GROUPS = 56
 
 
 def width(tokens):
@@ -50,18 +48,29 @@ def tile_picked_lrn8_none_p_kernel(tc, x_words, x_scales, w1, gn, w2, offs, p1, 
         scale_table = held.tile([P, T], U8, name="scale_table")
         nc.gpsimd.memset(scale_table[:].bitcast(I32), 0)
 
+        warm = held.tile([P, 2], F32, name="warm")
+        nc.gpsimd.memset(warm[:, 0:1], 1.0)
+        nc.scalar.activation(out=warm[:, 1:2], in_=warm[:, 0:1], func=ACT.Abs_reciprocal_sqrt, scale=0.5, bias=1.0)
+
         w1_raw = [held.tile([P, PACK, H], F32, name="w1_raw%d" % g) for g in range(PASSES)]
-        nc.sync.dma_start(w1_raw[0][:], w1[0:K_PASS, :].rearrange("(p j) c -> p j c", j=PACK))
+        word_table = [held.tile([P, T], I32, name="word_table%d" % g) for g in range(PASSES)]
+
+        def load_w1(g):
+            nc.sync.dma_start(w1_raw[g][:], w1[K_PASS * g : K_PASS * (g + 1), :].rearrange("(p j) c -> p j c", j=PACK))
+
+        def load_words(g):
+            nc.sync.dma_start(word_table[g][:], x_words[g].rearrange("p n j -> p (n j)").bitcast(I32))
+
+        load_w1(0)
         for quad in range(P // QUADRANT):
             nc.sync.dma_start(
                 scale_table[QUADRANT * quad : QUADRANT * quad + SCALE_ROWS * PASSES, :].bitcast(I32),
                 x_scales[:, SCALE_ROWS * quad : SCALE_ROWS * (quad + 1), :].bitcast(I32),
             )
         nc.sync.dma_start(picked[:], offs)
-        nc.sync.dma_start(w1_raw[1][:], w1[K_PASS : 2 * K_PASS, :].rearrange("(p j) c -> p j c", j=PACK))
-        word_table = [held.tile([P, T], I32, name="word_table%d" % g) for g in range(PASSES)]
-        for g in range(PASSES):
-            nc.sync.dma_start(word_table[g][:], x_words[g].rearrange("p n j -> p (n j)").bitcast(I32))
+        load_words(0)
+        load_w1(1)
+        load_words(1)
         nc.sync.dma_start(places[0][:], p1)
         nc.sync.dma_start(places[1][:], p2)
         gain = held.tile([P, PACK], F32, name="gain")
@@ -69,20 +78,16 @@ def tile_picked_lrn8_none_p_kernel(tc, x_words, x_scales, w1, gn, w2, offs, p1, 
         w2_raw = held.tile([P, PACK, N], F32, name="w2_raw")
         nc.sync.dma_start(w2_raw[:], w2.rearrange("(p j) c -> p j c", j=PACK))
 
-        w1_codes, w1_scales = [], []
-        for g in range(PASSES):
+        w1_codes = [held.tile([P, H], U32, name="w1_codes%d" % g, align_bytes=64) for g in range(PASSES)]
+        w1_scales = [held.tile([P, H], U8, name="w1_scales%d" % g, align_bytes=64) for g in range(PASSES)]
+
+        def quantise_w1(g):
             w1_grouped = held.tile([P, H * PACK], BF16, name="w1_grouped%d" % g, align_bytes=64)
             dst = w1_grouped[:].rearrange("p (t m j) -> p m j t", t=PACK, j=PACK)
             src = w1_raw[g][:].rearrange("p j (m t) -> p m j t", t=PACK)
             nc.scalar.copy(out=dst[:, 0:SCALAR_GROUPS], in_=src[:, 0:SCALAR_GROUPS])
             nc.vector.tensor_copy(out=dst[:, SCALAR_GROUPS:P], in_=src[:, SCALAR_GROUPS:P])
-            codes = held.tile([P, H], U32, name="w1_codes%d" % g, tag="w1_codes%d" % g, align_bytes=64)
-            scales = held.tile([P, H], U8, name="w1_scales%d" % g, align_bytes=64)
-            nc.vector.quantize_mx(out=codes[:].bitcast(FP8X4), scales=scales[:], in_=w1_grouped[:])
-            w1_codes.append(codes)
-            w1_scales.append(scales)
-        x_scale = held.tile([P, S], U8, name="x_scale", align_bytes=64)
-        nc.vector.tensor_copy(x_scale[:], scale_table[:].indirect(picked[:]))
+            nc.vector.quantize_mx(out=w1_codes[g][:].bitcast(FP8X4), scales=w1_scales[g][:], in_=w1_grouped[:])
 
         y = []
         for t in range(PACK):
@@ -94,42 +99,52 @@ def tile_picked_lrn8_none_p_kernel(tc, x_words, x_scales, w1, gn, w2, offs, p1, 
             part, bank = [entry for entry in y[t] if entry[0].start <= tokens.start < entry[0].stop][0]
             return bank[:, tokens.start - part.start : tokens.stop - part.start]
 
-        squares = [held.tile([P, S], F32, name="squares%d" % t) for t in range(PACK)]
+        x_scale = held.tile([P, S], U8, name="x_scale", align_bytes=64)
         x_codes = [held.tile([P, S], U32, name="x_codes%d" % g, align_bytes=64) for g in range(PASSES)]
 
-        def first_layer(t, g, start):
-            cols = slice(P * t, P * (t + 1))
-            for part, bank in y[t]:
-                nc.tensor.matmul_mx(
-                    out=bank[:],
-                    lhsT=w1_codes[g][:, cols].bitcast(FP8X4),
-                    lhsT_scale=w1_scales[g][:, cols],
-                    rhs=x_codes[g][:, part].bitcast(FP8X4),
-                    rhs_scale=x_scale[SCALE_ROWS * g : P, part],
-                    start=start,
-                    stop=not start,
-                )
+        def gather_words(g, tokens):
+            nc.vector.tensor_copy(
+                x_codes[g][:, tokens], word_table[g][:].bitcast(U32).indirect(picked[:, list_columns(tokens)])
+            )
 
-        for g in range(PASSES):
-            for part in HALVES if g == PASSES - 1 else (slice(0, S),):
-                nc.vector.tensor_copy(
-                    x_codes[g][:, part], word_table[g][:].bitcast(U32).indirect(picked[:, list_columns(part)])
-                )
-            for t in range(PACK - 1):
-                first_layer(t, g, g == 0)
-        first_layer(PACK - 1, 1, True)
-        first_layer(PACK - 1, 0, False)
+        def first_layer(g):
+            for t in range(PACK):
+                cols = slice(P * t, P * (t + 1))
+                for part, bank in y[t]:
+                    nc.tensor.matmul_mx(
+                        out=bank[:],
+                        lhsT=w1_codes[g][:, cols].bitcast(FP8X4),
+                        lhsT_scale=w1_scales[g][:, cols],
+                        rhs=x_codes[g][:, part].bitcast(FP8X4),
+                        rhs_scale=x_scale[SCALE_ROWS * g : P, part],
+                        start=g == 0,
+                        stop=g == PASSES - 1,
+                    )
 
-        last = CHUNKS[-1]
-        own = held.tile([P, PACK, last.start], F32, name="own")
-        own_last = [held.tile([P, width(last)], F32, name="own_last%d" % t) for t in range(PACK)]
-        gained = [held.tile([P, PACK, S // 2], F32, name="gained%d" % h, tag="gained%d" % h) for h in range(2)]
+        quantise_w1(0)
+        gather_words(0, slice(0, S))
+        nc.vector.tensor_copy(x_scale[:], scale_table[:].indirect(picked[:]))
+        first_layer(0)
+        quantise_w1(1)
+        for half in HALVES:
+            gather_words(1, half)
+        first_layer(1)
+
+        first, later = HALVES
+        everyone = slice(0, S)
+        windows = [held.tile([P, 2 * S if t < 2 else S], F32, name="window%d" % t) for t in range(PACK)]
+        for t in range(2):
+            nc.gpsimd.memset(windows[t][:, S : 2 * S], 0.0)
+        own = [held.tile([P, S], F32, name="own%d" % t) for t in range(PACK)]
         for t in range(PACK):
             for part, bank in y[t]:
-                nc.scalar.activation(out=squares[t][:, part], in_=bank[:], func=ACT.Square)
-                early = slice(part.start, min(part.stop, last.start))
-                nc.scalar.activation(out=own[:, t, early], in_=y_view(t, early), func=ACT.Square)
-            nc.sync.dma_start(own_last[t][:], squares[t][:, last])
+                nc.scalar.activation(out=windows[t][:, part], in_=bank[:], func=ACT.Square)
+                if t < 2:
+                    nc.scalar.activation(out=own[t][:, part], in_=bank[:], func=ACT.Square)
+            if t >= 2:
+                nc.sync.dma_start(own[t][:], windows[t][:, everyone])
+
+        gained = [held.tile([P, PACK, S // 2], F32, name="gained%d" % h, tag="gained%d" % h, align_bytes=64) for h in range(2)]
 
         def gain_y(h):
             for t in range(PACK):
@@ -137,66 +152,55 @@ def tile_picked_lrn8_none_p_kernel(tc, x_words, x_scales, w1, gn, w2, offs, p1, 
                     out=gained[h][:, t, :], in_=y_view(t, HALVES[h]), func=ACT.Copy, scale=gain[:, t : t + 1]
                 )
 
-        w2_grouped = held.tile([P, N * PACK], BF16, name="w2_grouped", tag="w1_codes1", align_bytes=64)
-        w2_codes = held.tile([P, N], U32, name="w2_codes", align_bytes=64)
+        w2_grouped = held.tile([P, N * PACK], BF16, name="w2_grouped", align_bytes=64)
         w2_scales = held.tile([P, N], U8, name="w2_scales", align_bytes=64)
 
-        def group_w2(half):
-            lines = slice(half * N // (2 * LINE), (half + 1) * N // (2 * LINE))
+        def group_w2():
             nc.scalar.copy(
-                out=w2_grouped[:].rearrange("p (c i j) -> p c j i", i=LINE, j=PACK)[:, lines],
-                in_=w2_raw[:].rearrange("p j (c i) -> p c j i", i=LINE)[:, lines],
+                out=w2_grouped[:].rearrange("p (c i j) -> p c j i", i=LINE, j=PACK),
+                in_=w2_raw[:].rearrange("p j (c i) -> p c j i", i=LINE),
             )
 
-        def quantise_w2(half):
-            cols = slice(half * N // 2, (half + 1) * N // 2)
-            nc.vector.quantize_mx(
-                out=w2_codes[:, cols].bitcast(FP8X4),
-                scales=w2_scales[:, cols],
-                in_=w2_grouped[:, PACK * cols.start : PACK * cols.stop],
-            )
+        partial = held.tile([P, PACK - 1, S], F32, name="partial")
+        roots = held.tile([P, PACK, S], F32, name="roots")
 
-        roots = [held.tile([P, PACK, width(ch)], F32, name="roots%d" % c) for c, ch in enumerate(CHUNKS)]
-        sums = [held.tile([P, PACK, width(ch)], F32, name="sums%d" % c) for c, ch in enumerate(CHUNKS)]
+        def add_first(dst, t, tokens):
+            looked_up = windows[t][:].indirect(places[0][:, list_columns(tokens)])
+            nc.vector.tensor_tensor(dst, looked_up, own[t][:, tokens], ALU.add)
 
-        def add_first(c, t, partial):
-            mine = own_last[t][:] if CHUNKS[c] == last else own[:, t, CHUNKS[c]]
-            looked_up = squares[t][:].indirect(places[0][:, list_columns(CHUNKS[c])])
-            nc.vector.tensor_tensor(partial[:, t, :], looked_up, mine, ALU.add)
+        def add_second(dst, t, tokens, src):
+            nc.vector.tensor_tensor(dst, windows[t][:].indirect(places[1][:, list_columns(tokens)]), src, ALU.add)
 
-        def add_second(c, t, partial):
-            looked_up = squares[t][:].indirect(places[1][:, list_columns(CHUNKS[c])])
-            nc.vector.tensor_tensor(sums[c][:, t, :], looked_up, partial[:, t, :], ALU.add)
+        def root(t, tokens, sums):
+            nc.scalar.activation(out=roots[:, t, tokens], in_=sums, func=ACT.Abs_reciprocal_sqrt, scale=0.5, bias=1.0)
 
-        def root(c):
-            for t in range(PACK):
-                nc.scalar.activation(
-                    out=roots[c][:, t, :], in_=sums[c][:, t, :], func=ACT.Abs_reciprocal_sqrt, scale=0.5, bias=1.0
-                )
-
-        z = [held.tile([P, width(ch) * PACK], BF16, name="z%d" % c, align_bytes=64) for c, ch in enumerate(CHUNKS)]
+        z = [
+            held.tile([P, width(ch) * PACK], BF16, name="z%d" % c, tag="z%d" % c, align_bytes=64)
+            for c, ch in enumerate(CHUNKS)
+        ]
 
         def normalise(c):
             h, lo = divmod(CHUNKS[c].start, S // 2)
             nc.vector.tensor_tensor(
                 z[c][:].rearrange("p (u i t) -> p u t i", i=LINE, t=PACK),
                 gained[h][:, :, lo : lo + width(CHUNKS[c])].rearrange("p t (u i) -> p u t i", i=LINE),
-                roots[c][:].rearrange("p t (u i) -> p u t i", i=LINE),
+                roots[:, :, CHUNKS[c]].rearrange("p t (u i) -> p u t i", i=LINE),
                 ALU.mult,
             )
 
-        out_tags = (("out0", "out1"), ("y0_0", "y1_0"), ("y0_256", "y2_0"))
+        out_tags = (("out0", "out1"), ("out2",), ("y0_0", "y1_0"))
 
-        def second_layer(c):
+        def second_layer(c, w2_codes):
             n = width(CHUNKS[c])
             z_codes = held.tile([P, n], U32, name="z_codes%d" % c, align_bytes=64)
             z_scales = held.tile([P, n], U8, name="z_scales%d" % c, align_bytes=64)
             nc.vector.quantize_mx(out=z_codes[:].bitcast(FP8X4), scales=z_scales[:], in_=z[c][:])
             banks = []
-            for b in range(OUT_BANKS):
-                bank = psum.tile([P, ROWS_PER_BANK // P, n], F32, name="out%d_%d" % (c, b), tag=out_tags[c][b])
-                for i in range(ROWS_PER_BANK // P):
-                    cols = slice(ROWS_PER_BANK * b + P * i, ROWS_PER_BANK * b + P * (i + 1))
+            blocks = N // P // len(out_tags[c])
+            for b, tag in enumerate(out_tags[c]):
+                bank = psum.tile([P, blocks, n], F32, name="out%d_%d" % (c, b), tag=tag)
+                for i in range(blocks):
+                    cols = slice(P * (blocks * b + i), P * (blocks * b + i + 1))
                     nc.tensor.matmul_mx(
                         out=bank[:, i, :],
                         lhsT=w2_codes[:, cols].bitcast(FP8X4),
@@ -210,40 +214,49 @@ def tile_picked_lrn8_none_p_kernel(tc, x_words, x_scales, w1, gn, w2, offs, p1, 
             return banks
 
         def store(c, banks, copies):
+            blocks = N // P // len(banks)
             for b, (bank, copy) in enumerate(zip(banks, copies)):
-                result = held.tile([P, ROWS_PER_BANK // P, width(CHUNKS[c])], F32, name="result%d_%d" % (c, b))
+                result = held.tile([P, blocks, width(CHUNKS[c])], F32, name="result%d_%d" % (c, b))
                 copy(out=result[:], in_=bank[:])
-                rows = out[ROWS_PER_BANK * b : ROWS_PER_BANK * (b + 1), CHUNKS[c]]
+                rows = out[P * blocks * b : P * blocks * (b + 1), CHUNKS[c]]
                 nc.sync.dma_start(rows.rearrange("(i p) n -> p i n", p=P), result[:])
 
-        partials = [held.tile([P, PACK, width(CHUNKS[c])], F32, name="partial%d" % c) for c in range(2)]
-        for t in range(PACK):
-            for c in range(2):
-                add_first(c, t, partials[c])
-            for c in range(2):
-                add_second(c, t, partials[c])
-        group_w2(0)
-        quantise_w2(0)
-        gain_y(0)
-        root(0)
-        group_w2(1)
-        normalise(0)
-        quantise_w2(1)
-        banks0 = second_layer(0)
+        for half in HALVES:
+            add_first(partial[:, 0, half], 0, half)
+        add_first(partial[:, 1, :], 1, everyone)
+        sums1 = held.tile([P, S], F32, name="sums1")
+        add_second(own[1][:], 0, everyone, partial[:, 0, :])
+        add_second(sums1[:], 1, everyone, partial[:, 1, :])
+        sums3 = held.tile([P, S // 2], F32, name="sums3")
+        add_first(partial[:, 2, first], 2, first)
+        add_first(partial[:, 2, later], 3, first)
+        add_second(own[3][:, first], 2, first, partial[:, 2, first])
+        add_second(sums3[:], 3, first, partial[:, 2, later])
+        add_first(partial[:, 2, later], 2, later)
+        add_first(partial[:, 2, first], 3, later)
 
-        partial_last = held.tile([P, PACK, width(last)], F32, name="partial2", tag="gained0")
-        add_first(2, 0, partial_last)
-        for t in range(1, PACK):
-            add_first(2, t, partial_last)
-            add_second(2, t - 1, partial_last)
-        add_second(2, PACK - 1, partial_last)
+        group_w2()
+        gain_y(0)
+        root(0, everyone, own[1][:])
+        root(1, everyone, sums1[:])
+        root(2, first, own[3][:, first])
+        root(3, first, sums3[:])
+        normalise(0)
+        w2_codes = held.tile([P, N], U32, name="w2_codes", tag="gained0", align_bytes=64)
+        nc.vector.quantize_mx(out=w2_codes[:].bitcast(FP8X4), scales=w2_scales[:], in_=w2_grouped[:])
+        banks0 = second_layer(0, w2_codes)
+
+        sums_later = held.tile([P, 2, S // 2], F32, name="sums_later", tag="z0", align_bytes=64)
+        add_second(sums_later[:, 0, :], 2, later, partial[:, 2, later])
+        add_second(sums_later[:, 1, :], 3, later, partial[:, 2, first])
         gain_y(1)
+        root(2, later, sums_later[:, 0, :])
+        for c in (1, 2):
+            root(3, CHUNKS[c], sums_later[:, 1, CHUNKS[c].start - later.start : CHUNKS[c].stop - later.start])
         store(0, banks0, (nc.scalar.copy, nc.scalar.copy))
-        root(1)
         normalise(1)
-        banks1 = second_layer(1)
-        root(2)
         normalise(2)
-        banks2 = second_layer(2)
-        store(1, banks1, (nc.scalar.copy, nc.vector.tensor_copy))
+        banks1 = second_layer(1, w2_codes)
+        banks2 = second_layer(2, w2_codes)
+        store(1, banks1, (nc.scalar.copy,))
         store(2, banks2, (nc.scalar.copy, nc.vector.tensor_copy))

@@ -24,8 +24,8 @@ QUADRANT = 32
 SCALE_ROWS = 4
 LINE = 4
 HALVES = (slice(0, S // 2), slice(S // 2, S))
-CHUNKS = (slice(0, 256), slice(256, 384), slice(384, 512))
-SCALAR_GROUPS = 56
+LAST_PIECES = (slice(256, 384), slice(384, 512))
+SCALAR_GROUPS = 48
 
 
 def width(tokens):
@@ -107,42 +107,43 @@ def tile_picked_lrn8_none_p_kernel(tc, x_words, x_scales, w1, gn, w2, offs, p1, 
                 x_codes[g][:, tokens], word_table[g][:].bitcast(U32).indirect(picked[:, list_columns(tokens)])
             )
 
-        def first_layer(g):
-            for t in range(PACK):
-                cols = slice(P * t, P * (t + 1))
-                for part, bank in y[t]:
-                    nc.tensor.matmul_mx(
-                        out=bank[:],
-                        lhsT=w1_codes[g][:, cols].bitcast(FP8X4),
-                        lhsT_scale=w1_scales[g][:, cols],
-                        rhs=x_codes[g][:, part].bitcast(FP8X4),
-                        rhs_scale=x_scale[SCALE_ROWS * g : P, part],
-                        start=g == 0,
-                        stop=g == PASSES - 1,
-                    )
+        def first_layer(t, g, start):
+            cols = slice(P * t, P * (t + 1))
+            for part, bank in y[t]:
+                nc.tensor.matmul_mx(
+                    out=bank[:],
+                    lhsT=w1_codes[g][:, cols].bitcast(FP8X4),
+                    lhsT_scale=w1_scales[g][:, cols],
+                    rhs=x_codes[g][:, part].bitcast(FP8X4),
+                    rhs_scale=x_scale[SCALE_ROWS * g : P, part],
+                    start=start,
+                    stop=not start,
+                )
 
         quantise_w1(0)
-        gather_words(0, slice(0, S))
         nc.vector.tensor_copy(x_scale[:], scale_table[:].indirect(picked[:]))
-        first_layer(0)
+        gather_words(0, slice(0, S))
+        for t in range(PACK):
+            first_layer(t, 0, True)
         quantise_w1(1)
         for half in HALVES:
             gather_words(1, half)
-        first_layer(1)
+        for t in range(PACK):
+            first_layer(t, 1, False)
 
         first, later = HALVES
         everyone = slice(0, S)
-        windows = [held.tile([P, 2 * S if t < 2 else S], F32, name="window%d" % t) for t in range(PACK)]
-        for t in range(2):
-            nc.gpsimd.memset(windows[t][:, S : 2 * S], 0.0)
-        own = [held.tile([P, S], F32, name="own%d" % t) for t in range(PACK)]
+        windows = [held.tile([P, 2 * S if t in (1, 2) else S], F32, name="window%d" % t) for t in range(PACK)]
+        own0 = held.tile([P, S], F32, name="own0")
+        own3 = held.tile([P, S], F32, name="own3", tag="own3", align_bytes=64)
+        own = [own0[:], windows[2][:, S : 2 * S], windows[1][:, S : 2 * S], own3[:]]
         for t in range(PACK):
             for part, bank in y[t]:
                 nc.scalar.activation(out=windows[t][:, part], in_=bank[:], func=ACT.Square)
-                if t < 2:
+                if t < PACK - 1:
                     nc.scalar.activation(out=own[t][:, part], in_=bank[:], func=ACT.Square)
-            if t >= 2:
-                nc.sync.dma_start(own[t][:], windows[t][:, everyone])
+        nc.sync.dma_start(own3[:], windows[3][:])
+        second_windows = [own0, windows[1], windows[2], windows[3]]
 
         gained = [held.tile([P, PACK, S // 2], F32, name="gained%d" % h, tag="gained%d" % h, align_bytes=64) for h in range(2)]
 
@@ -161,102 +162,116 @@ def tile_picked_lrn8_none_p_kernel(tc, x_words, x_scales, w1, gn, w2, offs, p1, 
                 in_=w2_raw[:].rearrange("p j (c i) -> p c j i", i=LINE),
             )
 
-        partial = held.tile([P, PACK - 1, S], F32, name="partial")
+        partial = held.tile([P, PACK, S], F32, name="partial")
+        sums = held.tile([P, PACK - 1, S], F32, name="sums")
         roots = held.tile([P, PACK, S], F32, name="roots")
 
-        def add_first(dst, t, tokens):
+        def add_first(t, tokens):
             looked_up = windows[t][:].indirect(places[0][:, list_columns(tokens)])
-            nc.vector.tensor_tensor(dst, looked_up, own[t][:, tokens], ALU.add)
+            nc.vector.tensor_tensor(partial[:, t, tokens], looked_up, own[t][:, tokens], ALU.add)
 
-        def add_second(dst, t, tokens, src):
-            nc.vector.tensor_tensor(dst, windows[t][:].indirect(places[1][:, list_columns(tokens)]), src, ALU.add)
+        def add_second(dst, t, tokens):
+            looked_up = second_windows[t][:].indirect(places[1][:, list_columns(tokens)])
+            nc.vector.tensor_tensor(dst, looked_up, partial[:, t, tokens], ALU.add)
 
-        def root(t, tokens, sums):
-            nc.scalar.activation(out=roots[:, t, tokens], in_=sums, func=ACT.Abs_reciprocal_sqrt, scale=0.5, bias=1.0)
+        def root(t, tokens, src):
+            nc.scalar.activation(out=roots[:, t, tokens], in_=src, func=ACT.Abs_reciprocal_sqrt, scale=0.5, bias=1.0)
 
-        z = [
-            held.tile([P, width(ch) * PACK], BF16, name="z%d" % c, tag="z%d" % c, align_bytes=64)
-            for c, ch in enumerate(CHUNKS)
-        ]
+        z = [held.tile([P, S // 2 * PACK], BF16, name="z%d" % h, align_bytes=64) for h in range(2)]
+        z_codes = [held.tile([P, S // 2], U32, name="z_codes%d" % h, align_bytes=64) for h in range(2)]
+        z_scales = [held.tile([P, S // 2], U8, name="z_scales%d" % h, align_bytes=64) for h in range(2)]
 
-        def normalise(c):
-            h, lo = divmod(CHUNKS[c].start, S // 2)
+        def normalise(tokens):
+            h, lo = divmod(tokens.start, S // 2)
+            hi = lo + width(tokens)
             nc.vector.tensor_tensor(
-                z[c][:].rearrange("p (u i t) -> p u t i", i=LINE, t=PACK),
-                gained[h][:, :, lo : lo + width(CHUNKS[c])].rearrange("p t (u i) -> p u t i", i=LINE),
-                roots[:, :, CHUNKS[c]].rearrange("p t (u i) -> p u t i", i=LINE),
+                z[h][:, PACK * lo : PACK * hi].rearrange("p (u i t) -> p u t i", i=LINE, t=PACK),
+                gained[h][:, :, lo:hi].rearrange("p t (u i) -> p u t i", i=LINE),
+                roots[:, :, tokens].rearrange("p t (u i) -> p u t i", i=LINE),
                 ALU.mult,
             )
 
-        out_tags = (("out0", "out1"), ("out2",), ("y0_0", "y1_0"))
+        def out_banks(h, tags):
+            shape = [P, N // P // len(tags), S // 2]
+            return [psum.tile(shape, F32, name="out%d_%d" % (h, b), tag=tag) for b, tag in enumerate(tags)]
 
-        def second_layer(c, w2_codes):
-            n = width(CHUNKS[c])
-            z_codes = held.tile([P, n], U32, name="z_codes%d" % c, align_bytes=64)
-            z_scales = held.tile([P, n], U8, name="z_scales%d" % c, align_bytes=64)
-            nc.vector.quantize_mx(out=z_codes[:].bitcast(FP8X4), scales=z_scales[:], in_=z[c][:])
-            banks = []
-            blocks = N // P // len(out_tags[c])
-            for b, tag in enumerate(out_tags[c]):
-                bank = psum.tile([P, blocks, n], F32, name="out%d_%d" % (c, b), tag=tag)
-                for i in range(blocks):
-                    cols = slice(P * (blocks * b + i), P * (blocks * b + i + 1))
-                    nc.tensor.matmul_mx(
-                        out=bank[:, i, :],
-                        lhsT=w2_codes[:, cols].bitcast(FP8X4),
-                        lhsT_scale=w2_scales[:, cols],
-                        rhs=z_codes[:].bitcast(FP8X4),
-                        rhs_scale=z_scales[:],
-                        start=True,
-                        stop=True,
-                    )
-                banks.append(bank)
-            return banks
+        def second_layer(tokens, banks):
+            h, lo = divmod(tokens.start, S // 2)
+            mine = slice(lo, lo + width(tokens))
+            nc.vector.quantize_mx(
+                out=z_codes[h][:, mine].bitcast(FP8X4),
+                scales=z_scales[h][:, mine],
+                in_=z[h][:, PACK * mine.start : PACK * mine.stop],
+            )
+            for block in range(N // P):
+                b, i = divmod(block, N // P // len(banks))
+                cols = slice(P * block, P * (block + 1))
+                nc.tensor.matmul_mx(
+                    out=banks[b][:, i, mine],
+                    lhsT=w2_codes[:, cols].bitcast(FP8X4),
+                    lhsT_scale=w2_scales[:, cols],
+                    rhs=z_codes[h][:, mine].bitcast(FP8X4),
+                    rhs_scale=z_scales[h][:, mine],
+                    start=True,
+                    stop=True,
+                )
 
-        def store(c, banks, copies):
+        def store(h, banks, b, copy):
             blocks = N // P // len(banks)
-            for b, (bank, copy) in enumerate(zip(banks, copies)):
-                result = held.tile([P, blocks, width(CHUNKS[c])], F32, name="result%d_%d" % (c, b))
-                copy(out=result[:], in_=bank[:])
-                rows = out[P * blocks * b : P * blocks * (b + 1), CHUNKS[c]]
-                nc.sync.dma_start(rows.rearrange("(i p) n -> p i n", p=P), result[:])
+            result = held.tile([P, blocks, S // 2], F32, name="result%d_%d" % (h, b))
+            copy(out=result[:], in_=banks[b][:])
+            rows = out[P * blocks * b : P * blocks * (b + 1), HALVES[h]]
+            nc.sync.dma_start(rows.rearrange("(i p) n -> p i n", p=P), result[:])
+
+        def raise_clock(name):
+            idle = psum.tile([P, S], F32, name=name, tag="out2")
+            nc.tensor.matmul_mx(
+                out=idle[:],
+                lhsT=w2_codes[:, 0:P].bitcast(FP8X4),
+                lhsT_scale=w2_scales[:, 0:P],
+                rhs=x_codes[0][:].bitcast(FP8X4),
+                rhs_scale=x_scale[:],
+                start=True,
+                stop=True,
+            )
 
         for half in HALVES:
-            add_first(partial[:, 0, half], 0, half)
-        add_first(partial[:, 1, :], 1, everyone)
-        sums1 = held.tile([P, S], F32, name="sums1")
-        add_second(own[1][:], 0, everyone, partial[:, 0, :])
-        add_second(sums1[:], 1, everyone, partial[:, 1, :])
+            add_first(0, half)
+        for half in HALVES:
+            add_second(sums[:, 0, half], 0, half)
+        for t in (1, 2):
+            add_first(t, everyone)
+        for t in (1, 2):
+            add_second(sums[:, t, :], t, everyone)
+        for half in HALVES:
+            add_first(3, half)
         sums3 = held.tile([P, S // 2], F32, name="sums3")
-        add_first(partial[:, 2, first], 2, first)
-        add_first(partial[:, 2, later], 3, first)
-        add_second(own[3][:, first], 2, first, partial[:, 2, first])
-        add_second(sums3[:], 3, first, partial[:, 2, later])
-        add_first(partial[:, 2, later], 2, later)
-        add_first(partial[:, 2, first], 3, later)
+        add_second(sums3[:], 3, first)
 
+        early_tiles = slice(0, PACK - 1)
         group_w2()
         gain_y(0)
-        root(0, everyone, own[1][:])
-        root(1, everyone, sums1[:])
-        root(2, first, own[3][:, first])
+        root(early_tiles, everyone, sums[:])
         root(3, first, sums3[:])
-        normalise(0)
-        w2_codes = held.tile([P, N], U32, name="w2_codes", tag="gained0", align_bytes=64)
-        nc.vector.quantize_mx(out=w2_codes[:].bitcast(FP8X4), scales=w2_scales[:], in_=w2_grouped[:])
-        banks0 = second_layer(0, w2_codes)
-
-        sums_later = held.tile([P, 2, S // 2], F32, name="sums_later", tag="z0", align_bytes=64)
-        add_second(sums_later[:, 0, :], 2, later, partial[:, 2, later])
-        add_second(sums_later[:, 1, :], 3, later, partial[:, 2, first])
         gain_y(1)
-        root(2, later, sums_later[:, 0, :])
-        for c in (1, 2):
-            root(3, CHUNKS[c], sums_later[:, 1, CHUNKS[c].start - later.start : CHUNKS[c].stop - later.start])
-        store(0, banks0, (nc.scalar.copy, nc.scalar.copy))
-        normalise(1)
-        normalise(2)
-        banks1 = second_layer(1, w2_codes)
-        banks2 = second_layer(2, w2_codes)
-        store(1, banks1, (nc.scalar.copy,))
-        store(2, banks2, (nc.scalar.copy, nc.vector.tensor_copy))
+        w2_codes = held.tile([P, N], U32, name="w2_codes", tag="own3", align_bytes=64)
+        nc.vector.quantize_mx(out=w2_codes[:].bitcast(FP8X4), scales=w2_scales[:], in_=w2_grouped[:])
+        for name in ("idle0", "idle1"):
+            raise_clock(name)
+        normalise(first)
+        pieces = [sums3[:, piece.start - later.start : piece.stop - later.start] for piece in LAST_PIECES]
+        add_second(pieces[0], 3, LAST_PIECES[0])
+        banks = out_banks(0, ("out0", "out1"))
+        second_layer(first, banks)
+        add_second(pieces[1], 3, LAST_PIECES[1])
+        for piece, src in zip(LAST_PIECES, pieces):
+            root(3, piece, src)
+        for b in range(len(banks)):
+            store(0, banks, b, nc.scalar.copy)
+        for piece in LAST_PIECES:
+            normalise(piece)
+        banks = out_banks(1, ("out2", "y0_0", "y0_256", "y1_0"))
+        for piece in LAST_PIECES:
+            second_layer(piece, banks)
+        for b in range(len(banks)):
+            store(1, banks, b, nc.vector.tensor_copy if b % 2 else nc.scalar.copy)

@@ -45,8 +45,9 @@ def tile_picked_lrn8_none_p_kernel(tc, x_words, x_scales, w1, gn, w2, offs, p1, 
         picked = held.tile([P, S // LIST_COLUMN], U16, name="picked")
         places = [held.tile([P, S // LIST_COLUMN], U16, name="places%d" % a) for a in range(2)]
 
-        scale_table = held.tile([P, T], U8, name="scale_table")
-        nc.gpsimd.memset(scale_table[:].bitcast(I32), 0)
+        scale_table = [held.tile([P, T], U8, name="scale_table%d" % g) for g in range(PASSES)]
+        for g in range(PASSES):
+            nc.gpsimd.memset(scale_table[g][:].bitcast(I32), 0)
 
         warm = held.tile([P, 2], F32, name="warm")
         nc.gpsimd.memset(warm[:, 0:1], 1.0)
@@ -61,15 +62,19 @@ def tile_picked_lrn8_none_p_kernel(tc, x_words, x_scales, w1, gn, w2, offs, p1, 
         def load_words(g):
             nc.sync.dma_start(word_table[g][:], x_words[g].rearrange("p n j -> p (n j)").bitcast(I32))
 
+        def load_scale_rows(g):
+            for r in range(SCALE_ROWS):
+                nc.sync.dma_start(
+                    scale_table[g][SCALE_ROWS * g + r : P : QUADRANT, :].bitcast(I32),
+                    x_scales[g, r : SCALE_ROWS * P // QUADRANT : SCALE_ROWS, :].bitcast(I32),
+                )
+
         load_w1(0)
-        for quad in range(P // QUADRANT):
-            nc.sync.dma_start(
-                scale_table[QUADRANT * quad : QUADRANT * quad + SCALE_ROWS * PASSES, :].bitcast(I32),
-                x_scales[:, SCALE_ROWS * quad : SCALE_ROWS * (quad + 1), :].bitcast(I32),
-            )
+        load_scale_rows(0)
         nc.sync.dma_start(picked[:], offs)
-        load_words(0)
         load_w1(1)
+        load_words(0)
+        load_scale_rows(1)
         load_words(1)
         nc.sync.dma_start(places[0][:], p1)
         nc.sync.dma_start(places[1][:], p2)
@@ -99,7 +104,7 @@ def tile_picked_lrn8_none_p_kernel(tc, x_words, x_scales, w1, gn, w2, offs, p1, 
             part, bank = [entry for entry in y[t] if entry[0].start <= tokens.start < entry[0].stop][0]
             return bank[:, tokens.start - part.start : tokens.stop - part.start]
 
-        x_scale = held.tile([P, S], U8, name="x_scale", align_bytes=64)
+        x_scale = [held.tile([P, S], U8, name="x_scale%d" % g, align_bytes=64) for g in range(PASSES)]
         x_codes = [held.tile([P, S], U32, name="x_codes%d" % g, align_bytes=64) for g in range(PASSES)]
 
         def gather_words(g, tokens):
@@ -115,21 +120,24 @@ def tile_picked_lrn8_none_p_kernel(tc, x_words, x_scales, w1, gn, w2, offs, p1, 
                     lhsT=w1_codes[g][:, cols].bitcast(FP8X4),
                     lhsT_scale=w1_scales[g][:, cols],
                     rhs=x_codes[g][:, part].bitcast(FP8X4),
-                    rhs_scale=x_scale[SCALE_ROWS * g : P, part],
+                    rhs_scale=x_scale[g][SCALE_ROWS * g : P, part],
                     start=start,
                     stop=not start,
                 )
 
         quantise_w1(0)
-        nc.vector.tensor_copy(x_scale[:], scale_table[:].indirect(picked[:]))
-        gather_words(0, slice(0, S))
-        for t in range(PACK):
-            first_layer(t, 0, True)
+        nc.vector.tensor_copy(x_scale[0][:], scale_table[0][:].indirect(picked[:]))
         quantise_w1(1)
+        gather_words(0, slice(0, S))
+        for t in range(PACK - 1):
+            first_layer(t, 0, True)
+        nc.vector.tensor_copy(x_scale[1][:], scale_table[1][:].indirect(picked[:]))
         for half in HALVES:
             gather_words(1, half)
-        for t in range(PACK):
+        for t in range(PACK - 1):
             first_layer(t, 1, False)
+        first_layer(PACK - 1, 1, True)
+        first_layer(PACK - 1, 0, False)
 
         first, later = HALVES
         everyone = slice(0, S)
@@ -230,7 +238,7 @@ def tile_picked_lrn8_none_p_kernel(tc, x_words, x_scales, w1, gn, w2, offs, p1, 
                 lhsT=w2_codes[:, 0:P].bitcast(FP8X4),
                 lhsT_scale=w2_scales[:, 0:P],
                 rhs=x_codes[0][:].bitcast(FP8X4),
-                rhs_scale=x_scale[:],
+                rhs_scale=x_scale[0][:],
                 start=True,
                 stop=True,
             )

@@ -53,6 +53,10 @@ def tile_picked_lrn8_none_p_kernel(tc, x_words, x_scales, w1, gn, w2, offs, p1, 
         nc.gpsimd.memset(warm[:, 0:1], 1.0)
         nc.scalar.activation(out=warm[:, 1:2], in_=warm[:, 0:1], func=ACT.Abs_reciprocal_sqrt, scale=0.5, bias=1.0)
 
+        windows = [held.tile([P, 2 * S if t in (1, 2) else S], F32, name="window%d" % t) for t in range(PACK)]
+        for t in (1, 2):
+            nc.gpsimd.memset(windows[t][:, S : 2 * S], 0.0)
+
         w1_raw = [held.tile([P, PACK, H], F32, name="w1_raw%d" % g) for g in range(PASSES)]
         word_table = [held.tile([P, T], I32, name="word_table%d" % g) for g in range(PASSES)]
 
@@ -141,17 +145,20 @@ def tile_picked_lrn8_none_p_kernel(tc, x_words, x_scales, w1, gn, w2, offs, p1, 
 
         first, later = HALVES
         everyone = slice(0, S)
-        windows = [held.tile([P, 2 * S if t in (1, 2) else S], F32, name="window%d" % t) for t in range(PACK)]
         own0 = held.tile([P, S], F32, name="own0")
+        own1 = held.tile([P, 2 * S], F32, name="own1")
         own3 = held.tile([P, S], F32, name="own3", tag="own3", align_bytes=64)
-        own = [own0[:], windows[2][:, S : 2 * S], windows[1][:, S : 2 * S], own3[:]]
+        fetched = own1[:, S : 2 * S]
+        own = [own0[:], own1[:, 0:S], None, own3[:]]
         for t in range(PACK):
             for part, bank in y[t]:
                 nc.scalar.activation(out=windows[t][:, part], in_=bank[:], func=ACT.Square)
-                if t < PACK - 1:
+                if own[t] is None:
+                    nc.scalar.activation(out=fetched, in_=windows[t][:].indirect(places[0][:]), func=ACT.Copy)
+                elif t < PACK - 1:
                     nc.scalar.activation(out=own[t][:, part], in_=bank[:], func=ACT.Square)
         nc.sync.dma_start(own3[:], windows[3][:])
-        second_windows = [own0, windows[1], windows[2], windows[3]]
+        second_windows = [own0, own1, windows[2], windows[3]]
 
         gained = [held.tile([P, PACK, S // 2], F32, name="gained%d" % h, tag="gained%d" % h, align_bytes=64) for h in range(2)]
 
@@ -247,10 +254,10 @@ def tile_picked_lrn8_none_p_kernel(tc, x_words, x_scales, w1, gn, w2, offs, p1, 
             add_first(0, half)
         for half in HALVES:
             add_second(sums[:, 0, half], 0, half)
-        for t in (1, 2):
-            add_first(t, everyone)
-        for t in (1, 2):
-            add_second(sums[:, t, :], t, everyone)
+        add_first(1, everyone)
+        nc.vector.tensor_tensor(partial[:, 2, :], windows[2][:].indirect(places[1][:]), fetched, ALU.add)
+        add_second(sums[:, 1, :], 1, everyone)
+        nc.vector.tensor_tensor(sums[:, 2, :], partial[:, 2, :], windows[2][:, everyone], ALU.add)
         for half in HALVES:
             add_first(3, half)
         sums3 = held.tile([P, S // 2], F32, name="sums3")

@@ -45,9 +45,8 @@ def tile_picked_lrn8_none_p_kernel(tc, x_words, x_scales, w1, gn, w2, offs, p1, 
         picked = held.tile([P, S // LIST_COLUMN], U16, name="picked")
         places = [held.tile([P, S // LIST_COLUMN], U16, name="places%d" % a) for a in range(2)]
 
-        scale_table = [held.tile([P, T], U8, name="scale_table%d" % g) for g in range(PASSES)]
-        for g in range(PASSES):
-            nc.gpsimd.memset(scale_table[g][:].bitcast(I32), 0)
+        scale_table = held.tile([P, T], U8, name="scale_table")
+        nc.gpsimd.memset(scale_table[:].bitcast(I32), 0)
 
         warm = held.tile([P, 2], F32, name="warm")
         nc.gpsimd.memset(warm[:, 0:1], 1.0)
@@ -69,16 +68,16 @@ def tile_picked_lrn8_none_p_kernel(tc, x_words, x_scales, w1, gn, w2, offs, p1, 
         def load_scale_rows(g):
             for r in range(SCALE_ROWS):
                 nc.sync.dma_start(
-                    scale_table[g][SCALE_ROWS * g + r : P : QUADRANT, :].bitcast(I32),
+                    scale_table[SCALE_ROWS * g + r : P : QUADRANT, :].bitcast(I32),
                     x_scales[g, r : SCALE_ROWS * P // QUADRANT : SCALE_ROWS, :].bitcast(I32),
                 )
 
         load_w1(0)
         load_scale_rows(0)
         nc.sync.dma_start(picked[:], offs)
-        load_w1(1)
         load_words(0)
         load_scale_rows(1)
+        load_w1(1)
         load_words(1)
         nc.sync.dma_start(places[0][:], p1)
         nc.sync.dma_start(places[1][:], p2)
@@ -108,7 +107,7 @@ def tile_picked_lrn8_none_p_kernel(tc, x_words, x_scales, w1, gn, w2, offs, p1, 
             part, bank = [entry for entry in y[t] if entry[0].start <= tokens.start < entry[0].stop][0]
             return bank[:, tokens.start - part.start : tokens.stop - part.start]
 
-        x_scale = [held.tile([P, S], U8, name="x_scale%d" % g, align_bytes=64) for g in range(PASSES)]
+        x_scale = held.tile([P, S], U8, name="x_scale", align_bytes=64)
         x_codes = [held.tile([P, S], U32, name="x_codes%d" % g, align_bytes=64) for g in range(PASSES)]
 
         def gather_words(g, tokens):
@@ -124,24 +123,21 @@ def tile_picked_lrn8_none_p_kernel(tc, x_words, x_scales, w1, gn, w2, offs, p1, 
                     lhsT=w1_codes[g][:, cols].bitcast(FP8X4),
                     lhsT_scale=w1_scales[g][:, cols],
                     rhs=x_codes[g][:, part].bitcast(FP8X4),
-                    rhs_scale=x_scale[g][SCALE_ROWS * g : P, part],
+                    rhs_scale=x_scale[SCALE_ROWS * g : P, part],
                     start=start,
                     stop=not start,
                 )
 
         quantise_w1(0)
-        nc.vector.tensor_copy(x_scale[0][:], scale_table[0][:].indirect(picked[:]))
-        quantise_w1(1)
         gather_words(0, slice(0, S))
-        for t in range(PACK - 1):
+        nc.vector.tensor_copy(x_scale[:], scale_table[:].indirect(picked[:]))
+        for t in range(PACK):
             first_layer(t, 0, True)
-        nc.vector.tensor_copy(x_scale[1][:], scale_table[1][:].indirect(picked[:]))
+        quantise_w1(1)
         for half in HALVES:
             gather_words(1, half)
-        for t in range(PACK - 1):
+        for t in range(PACK):
             first_layer(t, 1, False)
-        first_layer(PACK - 1, 1, True)
-        first_layer(PACK - 1, 0, False)
 
         first, later = HALVES
         everyone = slice(0, S)
@@ -157,7 +153,9 @@ def tile_picked_lrn8_none_p_kernel(tc, x_words, x_scales, w1, gn, w2, offs, p1, 
                     nc.scalar.activation(out=fetched, in_=windows[t][:].indirect(places[0][:]), func=ACT.Copy)
                 elif t < PACK - 1:
                     nc.scalar.activation(out=own[t][:, part], in_=bank[:], func=ACT.Square)
-        nc.sync.dma_start(own3[:], windows[3][:])
+        nc.sync.dma_start(own3[:, later], windows[3][:, later])
+        looked_up = windows[3][:].indirect(places[0][:, list_columns(first)])
+        nc.scalar.activation(out=own3[:, first], in_=looked_up, func=ACT.Copy)
         second_windows = [own0, own1, windows[2], windows[3]]
 
         gained = [held.tile([P, PACK, S // 2], F32, name="gained%d" % h, tag="gained%d" % h, align_bytes=64) for h in range(2)]
@@ -210,15 +208,21 @@ def tile_picked_lrn8_none_p_kernel(tc, x_words, x_scales, w1, gn, w2, offs, p1, 
             shape = [P, N // P // len(tags), S // 2]
             return [psum.tile(shape, F32, name="out%d_%d" % (h, b), tag=tag) for b, tag in enumerate(tags)]
 
-        def second_layer(tokens, banks):
+        def within_half(tokens):
             h, lo = divmod(tokens.start, S // 2)
-            mine = slice(lo, lo + width(tokens))
+            return h, slice(lo, lo + width(tokens))
+
+        def quantise_z(tokens):
+            h, mine = within_half(tokens)
             nc.vector.quantize_mx(
                 out=z_codes[h][:, mine].bitcast(FP8X4),
                 scales=z_scales[h][:, mine],
                 in_=z[h][:, PACK * mine.start : PACK * mine.stop],
             )
-            for block in range(N // P):
+
+        def second_layer(tokens, banks, blocks):
+            h, mine = within_half(tokens)
+            for block in blocks:
                 b, i = divmod(block, N // P // len(banks))
                 cols = slice(P * block, P * (block + 1))
                 nc.tensor.matmul_mx(
@@ -238,14 +242,14 @@ def tile_picked_lrn8_none_p_kernel(tc, x_words, x_scales, w1, gn, w2, offs, p1, 
             rows = out[P * blocks * b : P * blocks * (b + 1), HALVES[h]]
             nc.sync.dma_start(rows.rearrange("(i p) n -> p i n", p=P), result[:])
 
-        def raise_clock(name):
-            idle = psum.tile([P, S], F32, name=name, tag="out2")
+        def raise_clock():
+            idle = psum.tile([P, H], F32, name="idle", tag="y3_0")
             nc.tensor.matmul_mx(
                 out=idle[:],
                 lhsT=w2_codes[:, 0:P].bitcast(FP8X4),
                 lhsT_scale=w2_scales[:, 0:P],
-                rhs=x_codes[0][:].bitcast(FP8X4),
-                rhs_scale=x_scale[0][:],
+                rhs=w1_codes[0][:].bitcast(FP8X4),
+                rhs_scale=w1_scales[0][:],
                 start=True,
                 stop=True,
             )
@@ -257,27 +261,29 @@ def tile_picked_lrn8_none_p_kernel(tc, x_words, x_scales, w1, gn, w2, offs, p1, 
         add_first(1, everyone)
         nc.vector.tensor_tensor(partial[:, 2, :], windows[2][:].indirect(places[1][:]), fetched, ALU.add)
         add_second(sums[:, 1, :], 1, everyone)
+        looked_up = windows[3][:].indirect(places[1][:, list_columns(first)])
+        nc.vector.tensor_tensor(partial[:, 3, first], looked_up, own3[:, first], ALU.add)
         nc.vector.tensor_tensor(sums[:, 2, :], partial[:, 2, :], windows[2][:, everyone], ALU.add)
-        for half in HALVES:
-            add_first(3, half)
         sums3 = held.tile([P, S // 2], F32, name="sums3")
-        add_second(sums3[:], 3, first)
+        nc.vector.tensor_tensor(sums3[:], partial[:, 3, first], windows[3][:, first], ALU.add)
+        add_first(3, later)
 
         early_tiles = slice(0, PACK - 1)
         group_w2()
         gain_y(0)
-        root(early_tiles, everyone, sums[:])
+        root(early_tiles, first, sums[:, :, first])
         root(3, first, sums3[:])
         gain_y(1)
+        root(early_tiles, later, sums[:, :, later])
         w2_codes = held.tile([P, N], U32, name="w2_codes", tag="own3", align_bytes=64)
         nc.vector.quantize_mx(out=w2_codes[:].bitcast(FP8X4), scales=w2_scales[:], in_=w2_grouped[:])
-        for name in ("idle0", "idle1"):
-            raise_clock(name)
+        raise_clock()
         normalise(first)
         pieces = [sums3[:, piece.start - later.start : piece.stop - later.start] for piece in LAST_PIECES]
         add_second(pieces[0], 3, LAST_PIECES[0])
         banks = out_banks(0, ("out0", "out1"))
-        second_layer(first, banks)
+        quantise_z(first)
+        second_layer(first, banks, range(N // P))
         add_second(pieces[1], 3, LAST_PIECES[1])
         for piece, src in zip(LAST_PIECES, pieces):
             root(3, piece, src)
@@ -287,6 +293,8 @@ def tile_picked_lrn8_none_p_kernel(tc, x_words, x_scales, w1, gn, w2, offs, p1, 
             normalise(piece)
         banks = out_banks(1, ("out2", "y0_0", "y0_256", "y1_0"))
         for piece in LAST_PIECES:
-            second_layer(piece, banks)
+            quantise_z(piece)
+            second_layer(piece, banks, (0, 1))
+        second_layer(later, banks, (2, 3))
         for b in range(len(banks)):
             store(1, banks, b, nc.vector.tensor_copy if b % 2 else nc.scalar.copy)

@@ -242,18 +242,6 @@ def tile_picked_lrn8_none_p_kernel(tc, x_words, x_scales, w1, gn, w2, offs, p1, 
             rows = out[P * blocks * b : P * blocks * (b + 1), HALVES[h]]
             nc.sync.dma_start(rows.rearrange("(i p) n -> p i n", p=P), result[:])
 
-        def raise_clock():
-            idle = psum.tile([P, H], F32, name="idle", tag="y3_0")
-            nc.tensor.matmul_mx(
-                out=idle[:],
-                lhsT=w2_codes[:, 0:P].bitcast(FP8X4),
-                lhsT_scale=w2_scales[:, 0:P],
-                rhs=w1_codes[0][:].bitcast(FP8X4),
-                rhs_scale=w1_scales[0][:],
-                start=True,
-                stop=True,
-            )
-
         for half in HALVES:
             add_first(0, half)
         for half in HALVES:
@@ -277,7 +265,6 @@ def tile_picked_lrn8_none_p_kernel(tc, x_words, x_scales, w1, gn, w2, offs, p1, 
         root(early_tiles, later, sums[:, :, later])
         w2_codes = held.tile([P, N], U32, name="w2_codes", tag="own3", align_bytes=64)
         nc.vector.quantize_mx(out=w2_codes[:].bitcast(FP8X4), scales=w2_scales[:], in_=w2_grouped[:])
-        raise_clock()
         normalise(first)
         pieces = [sums3[:, piece.start - later.start : piece.stop - later.start] for piece in LAST_PIECES]
         add_second(pieces[0], 3, LAST_PIECES[0])

@@ -24,7 +24,8 @@ QUADRANT = 32
 SCALE_ROWS = 4
 LINE = 4
 HALVES = (slice(0, S // 2), slice(S // 2, S))
-LAST_PIECES = (slice(256, 384), slice(384, 512))
+CHUNK = 128
+CHUNKS = tuple(slice(a, a + CHUNK) for a in range(0, S, CHUNK))
 SCALAR_GROUPS = 48
 
 
@@ -51,10 +52,6 @@ def tile_picked_lrn8_none_p_kernel(tc, x_words, x_scales, w1, gn, w2, offs, p1, 
         warm = held.tile([P, 2], F32, name="warm")
         nc.gpsimd.memset(warm[:, 0:1], 1.0)
         nc.scalar.activation(out=warm[:, 1:2], in_=warm[:, 0:1], func=ACT.Abs_reciprocal_sqrt, scale=0.5, bias=1.0)
-
-        windows = [held.tile([P, 2 * S if t in (1, 2) else S], F32, name="window%d" % t) for t in range(PACK)]
-        for t in (1, 2):
-            nc.gpsimd.memset(windows[t][:, S : 2 * S], 0.0)
 
         w1_raw = [held.tile([P, PACK, H], F32, name="w1_raw%d" % g) for g in range(PASSES)]
         word_table = [held.tile([P, T], I32, name="word_table%d" % g) for g in range(PASSES)]
@@ -115,7 +112,7 @@ def tile_picked_lrn8_none_p_kernel(tc, x_words, x_scales, w1, gn, w2, offs, p1, 
                 x_codes[g][:, tokens], word_table[g][:].bitcast(U32).indirect(picked[:, list_columns(tokens)])
             )
 
-        def first_layer(t, g, start):
+        def first_layer(t, g):
             cols = slice(P * t, P * (t + 1))
             for part, bank in y[t]:
                 nc.tensor.matmul_mx(
@@ -124,93 +121,90 @@ def tile_picked_lrn8_none_p_kernel(tc, x_words, x_scales, w1, gn, w2, offs, p1, 
                     lhsT_scale=w1_scales[g][:, cols],
                     rhs=x_codes[g][:, part].bitcast(FP8X4),
                     rhs_scale=x_scale[SCALE_ROWS * g : P, part],
-                    start=start,
-                    stop=not start,
+                    start=g == 0,
+                    stop=g == PASSES - 1,
                 )
 
         quantise_w1(0)
         gather_words(0, slice(0, S))
         nc.vector.tensor_copy(x_scale[:], scale_table[:].indirect(picked[:]))
         for t in range(PACK):
-            first_layer(t, 0, True)
+            first_layer(t, 0)
         quantise_w1(1)
         for half in HALVES:
             gather_words(1, half)
         for t in range(PACK):
-            first_layer(t, 1, False)
+            first_layer(t, 1)
 
         first, later = HALVES
-        everyone = slice(0, S)
-        own0 = held.tile([P, S], F32, name="own0")
-        own1 = held.tile([P, 2 * S], F32, name="own1")
-        own3 = held.tile([P, S], F32, name="own3", tag="own3", align_bytes=64)
-        fetched = own1[:, S : 2 * S]
-        own = [own0[:], own1[:, 0:S], None, own3[:]]
-        for t in range(PACK):
-            for part, bank in y[t]:
-                nc.scalar.activation(out=windows[t][:, part], in_=bank[:], func=ACT.Square)
-                if own[t] is None:
-                    nc.scalar.activation(out=fetched, in_=windows[t][:].indirect(places[0][:]), func=ACT.Copy)
-                elif t < PACK - 1:
-                    nc.scalar.activation(out=own[t][:, part], in_=bank[:], func=ACT.Square)
-        nc.sync.dma_start(own3[:, later], windows[3][:, later])
-        looked_up = windows[3][:].indirect(places[0][:, list_columns(first)])
-        nc.scalar.activation(out=own3[:, first], in_=looked_up, func=ACT.Copy)
-        second_windows = [own0, own1, windows[2], windows[3]]
+        windows = [held.tile([P, S], F32, name="window%d" % t) for t in range(PACK)]
+        addend = held.tile([P, PACK, S], F32, name="addend")
+        partial = held.tile([P, PACK, S], F32, name="partial")
+        sums = held.tile([P, PACK, S], F32, name="sums")
+        roots = held.tile([P, PACK, S], F32, name="roots")
+        planes = held.tile([P, PACK, S], BF16, name="planes")
 
-        gained = [held.tile([P, PACK, S // 2], F32, name="gained%d" % h, tag="gained%d" % h, align_bytes=64) for h in range(2)]
+        def square(dst, t, tokens):
+            nc.scalar.activation(out=dst[:, tokens], in_=y_view(t, tokens), func=ACT.Square)
 
-        def gain_y(h):
-            for t in range(PACK):
-                nc.scalar.activation(
-                    out=gained[h][:, t, :], in_=y_view(t, HALVES[h]), func=ACT.Copy, scale=gain[:, t : t + 1]
-                )
+        def look_up(t, a, tokens):
+            return windows[t][:].indirect(places[a][:, list_columns(tokens)])
 
-        w2_grouped = held.tile([P, N * PACK], BF16, name="w2_grouped", align_bytes=64)
-        w2_scales = held.tile([P, N], U8, name="w2_scales", align_bytes=64)
+        def fetch(t, tokens):
+            nc.scalar.activation(out=addend[:, t, tokens], in_=look_up(t, 0, tokens), func=ACT.Copy)
 
-        def group_w2():
-            nc.scalar.copy(
-                out=w2_grouped[:].rearrange("p (c i j) -> p c j i", i=LINE, j=PACK),
-                in_=w2_raw[:].rearrange("p j (c i) -> p c j i", i=LINE),
+        def first_add(t, tokens):
+            a = 0 if t == 0 else 1
+            nc.vector.tensor_tensor(partial[:, t, tokens], look_up(t, a, tokens), addend[:, t, tokens], ALU.add)
+
+        def second_add(t, tokens):
+            third = look_up(t, 1, tokens) if t == 0 else windows[t][:, tokens]
+            nc.vector.tensor_tensor(sums[:, t, tokens], third, partial[:, t, tokens], ALU.add)
+
+        def root(t, tokens):
+            nc.scalar.activation(
+                out=roots[:, t, tokens], in_=sums[:, t, tokens], func=ACT.Abs_reciprocal_sqrt, scale=0.5, bias=1.0
             )
 
-        partial = held.tile([P, PACK, S], F32, name="partial")
-        sums = held.tile([P, PACK - 1, S], F32, name="sums")
-        roots = held.tile([P, PACK, S], F32, name="roots")
+        def normalise(t, tokens):
+            nc.vector.scalar_tensor_tensor(
+                out=planes[:, t, tokens],
+                in0=y_view(t, tokens),
+                scalar=gain[:, t : t + 1],
+                in1=roots[:, t, tokens],
+                op0=ALU.mult,
+                op1=ALU.mult,
+            )
 
-        def add_first(t, tokens):
-            looked_up = windows[t][:].indirect(places[0][:, list_columns(tokens)])
-            nc.vector.tensor_tensor(partial[:, t, tokens], looked_up, own[t][:, tokens], ALU.add)
+        w2_grouped = held.tile([P, N * PACK], BF16, name="w2_grouped", align_bytes=64)
+        w2_codes = held.tile([P, N], U32, name="w2_codes", align_bytes=64)
+        w2_scales = held.tile([P, N], U8, name="w2_scales", align_bytes=64)
 
-        def add_second(dst, t, tokens):
-            looked_up = second_windows[t][:].indirect(places[1][:, list_columns(tokens)])
-            nc.vector.tensor_tensor(dst, looked_up, partial[:, t, tokens], ALU.add)
-
-        def root(t, tokens, src):
-            nc.scalar.activation(out=roots[:, t, tokens], in_=src, func=ACT.Abs_reciprocal_sqrt, scale=0.5, bias=1.0)
+        def group_w2(block):
+            cols = slice(P * block, P * (block + 1))
+            nc.scalar.copy(
+                out=w2_grouped[:, PACK * cols.start : PACK * cols.stop].rearrange("p (c i j) -> p c j i", i=LINE, j=PACK),
+                in_=w2_raw[:, :, cols].rearrange("p j (c i) -> p c j i", i=LINE),
+            )
 
         z = [held.tile([P, S // 2 * PACK], BF16, name="z%d" % h, align_bytes=64) for h in range(2)]
         z_codes = [held.tile([P, S // 2], U32, name="z_codes%d" % h, align_bytes=64) for h in range(2)]
         z_scales = [held.tile([P, S // 2], U8, name="z_scales%d" % h, align_bytes=64) for h in range(2)]
 
-        def normalise(tokens):
+        def within_half(tokens):
             h, lo = divmod(tokens.start, S // 2)
-            hi = lo + width(tokens)
-            nc.vector.tensor_tensor(
-                z[h][:, PACK * lo : PACK * hi].rearrange("p (u i t) -> p u t i", i=LINE, t=PACK),
-                gained[h][:, :, lo:hi].rearrange("p t (u i) -> p u t i", i=LINE),
-                roots[:, :, tokens].rearrange("p t (u i) -> p u t i", i=LINE),
-                ALU.mult,
+            return h, slice(lo, lo + width(tokens))
+
+        def group_z(tokens):
+            h, mine = within_half(tokens)
+            nc.vector.tensor_copy(
+                out=z[h][:, PACK * mine.start : PACK * mine.stop].rearrange("p (u i t) -> p u t i", i=LINE, t=PACK),
+                in_=planes[:, :, tokens].rearrange("p t (u i) -> p u t i", i=LINE),
             )
 
         def out_banks(h, tags):
             shape = [P, N // P // len(tags), S // 2]
             return [psum.tile(shape, F32, name="out%d_%d" % (h, b), tag=tag) for b, tag in enumerate(tags)]
-
-        def within_half(tokens):
-            h, lo = divmod(tokens.start, S // 2)
-            return h, slice(lo, lo + width(tokens))
 
         def quantise_z(tokens):
             h, mine = within_half(tokens)
@@ -242,44 +236,52 @@ def tile_picked_lrn8_none_p_kernel(tc, x_words, x_scales, w1, gn, w2, offs, p1, 
             rows = out[P * blocks * b : P * blocks * (b + 1), HALVES[h]]
             nc.sync.dma_start(rows.rearrange("(i p) n -> p i n", p=P), result[:])
 
+        last = PACK - 1
+        for t in range(last):
+            for part, bank in y[t]:
+                square(windows[t], t, part)
+                if t == 0:
+                    square(addend[:, 0, :], t, part)
+            if t > 0:
+                for half in HALVES:
+                    fetch(t, half)
+            for half in HALVES:
+                first_add(t, half)
+            for half in HALVES:
+                second_add(t, half)
+        square(windows[last], last, slice(0, S))
         for half in HALVES:
-            add_first(0, half)
-        for half in HALVES:
-            add_second(sums[:, 0, half], 0, half)
-        add_first(1, everyone)
-        nc.vector.tensor_tensor(partial[:, 2, :], windows[2][:].indirect(places[1][:]), fetched, ALU.add)
-        add_second(sums[:, 1, :], 1, everyone)
-        looked_up = windows[3][:].indirect(places[1][:, list_columns(first)])
-        nc.vector.tensor_tensor(partial[:, 3, first], looked_up, own3[:, first], ALU.add)
-        nc.vector.tensor_tensor(sums[:, 2, :], partial[:, 2, :], windows[2][:, everyone], ALU.add)
-        sums3 = held.tile([P, S // 2], F32, name="sums3")
-        nc.vector.tensor_tensor(sums3[:], partial[:, 3, first], windows[3][:, first], ALU.add)
-        add_first(3, later)
-
-        early_tiles = slice(0, PACK - 1)
-        group_w2()
-        gain_y(0)
-        root(early_tiles, first, sums[:, :, first])
-        root(3, first, sums3[:])
-        gain_y(1)
-        root(early_tiles, later, sums[:, :, later])
-        w2_codes = held.tile([P, N], U32, name="w2_codes", tag="own3", align_bytes=64)
+            fetch(last, half)
+        root(0, first)
+        root(1, first)
+        group_w2(0)
+        group_w2(1)
+        first_add(last, first)
+        normalise(0, first)
+        second_add(last, first)
+        first_add(last, later)
+        root(2, first)
+        root(last, first)
+        group_w2(2)
+        group_w2(3)
+        for t in range(1, PACK):
+            normalise(t, first)
+        second_add(last, later)
+        group_z(first)
+        for t in range(PACK):
+            root(t, later)
         nc.vector.quantize_mx(out=w2_codes[:].bitcast(FP8X4), scales=w2_scales[:], in_=w2_grouped[:])
-        normalise(first)
-        pieces = [sums3[:, piece.start - later.start : piece.stop - later.start] for piece in LAST_PIECES]
-        add_second(pieces[0], 3, LAST_PIECES[0])
-        banks = out_banks(0, ("out0", "out1"))
         quantise_z(first)
+        banks = out_banks(0, ("out0", "out1"))
         second_layer(first, banks, range(N // P))
-        add_second(pieces[1], 3, LAST_PIECES[1])
-        for piece, src in zip(LAST_PIECES, pieces):
-            root(3, piece, src)
+        for t in range(PACK):
+            normalise(t, later)
         for b in range(len(banks)):
             store(0, banks, b, nc.scalar.copy)
-        for piece in LAST_PIECES:
-            normalise(piece)
+        for piece in CHUNKS[2:]:
+            group_z(piece)
         banks = out_banks(1, ("out2", "y0_0", "y0_256", "y1_0"))
-        for piece in LAST_PIECES:
+        for piece in CHUNKS[2:]:
             quantise_z(piece)
             second_layer(piece, banks, (0, 1))
         second_layer(later, banks, (2, 3))

@@ -1,6 +1,7 @@
 from contextlib import ExitStack
 
 import concourse.mybir as mybir
+from concourse.masks import make_identity
 
 K, T, S, N, H = 1024, 2048, 512, 512, 512
 FLOPS = 2 * K * H * S + 2 * H * N * S
@@ -52,6 +53,12 @@ def tile_picked_lrn8_none_p_kernel(tc, x_words, x_scales, w1, gn, w2, offs, p1, 
         warm = held.tile([P, 2], F32, name="warm")
         nc.gpsimd.memset(warm[:, 0:1], 1.0)
         nc.scalar.activation(out=warm[:, 1:2], in_=warm[:, 0:1], func=ACT.Abs_reciprocal_sqrt, scale=0.5, bias=1.0)
+
+        windows = [held.tile([P, 2 * S if t in (1, 2) else S], F32, name="window%d" % t) for t in range(PACK)]
+        for t in (1, 2):
+            nc.gpsimd.memset(windows[t][:, S : 2 * S], 0.0)
+        identity = held.tile([P, P], F32, name="identity")
+        make_identity(nc, identity[:])
 
         w1_raw = [held.tile([P, PACK, H], F32, name="w1_raw%d" % g) for g in range(PASSES)]
         word_table = [held.tile([P, T], I32, name="word_table%d" % g) for g in range(PASSES)]
@@ -137,55 +144,49 @@ def tile_picked_lrn8_none_p_kernel(tc, x_words, x_scales, w1, gn, w2, offs, p1, 
             first_layer(t, 1)
 
         first, later = HALVES
-        windows = [held.tile([P, S], F32, name="window%d" % t) for t in range(PACK)]
-        addend = held.tile([P, PACK, S], F32, name="addend")
-        partial = held.tile([P, PACK, S], F32, name="partial")
-        sums = held.tile([P, PACK, S], F32, name="sums")
-        roots = held.tile([P, PACK, S], F32, name="roots")
-        planes = held.tile([P, PACK, S], BF16, name="planes")
+        everyone = slice(0, S)
+        last = PACK - 1
+        gained = held.tile([P, PACK, S], F32, name="gained")
 
-        def square(dst, t, tokens):
-            nc.scalar.activation(out=dst[:, tokens], in_=y_view(t, tokens), func=ACT.Square)
+        def square(t, tokens):
+            nc.scalar.activation(out=windows[t][:, tokens], in_=y_view(t, tokens), func=ACT.Square)
+
+        def gain_y(t, tokens):
+            nc.scalar.activation(out=gained[:, t, tokens], in_=y_view(t, tokens), func=ACT.Copy, scale=gain[:, t : t + 1])
 
         def look_up(t, a, tokens):
             return windows[t][:].indirect(places[a][:, list_columns(tokens)])
 
-        def fetch(t, tokens):
-            nc.scalar.activation(out=addend[:, t, tokens], in_=look_up(t, 0, tokens), func=ACT.Copy)
+        def fetch_scalar(dst, t, tokens):
+            nc.scalar.activation(out=dst, in_=look_up(t, 0, tokens), func=ACT.Copy)
 
-        def first_add(t, tokens):
-            a = 0 if t == 0 else 1
-            nc.vector.tensor_tensor(partial[:, t, tokens], look_up(t, a, tokens), addend[:, t, tokens], ALU.add)
+        def fetch_vector(dst, t, tokens):
+            nc.vector.tensor_copy(dst, look_up(t, 0, tokens))
 
-        def second_add(t, tokens):
-            third = look_up(t, 1, tokens) if t == 0 else windows[t][:, tokens]
-            nc.vector.tensor_tensor(sums[:, t, tokens], third, partial[:, t, tokens], ALU.add)
+        def add_second(dst, t, tokens, fetched):
+            nc.vector.tensor_tensor(dst, look_up(t, 1, tokens), fetched, ALU.add)
 
-        def root(t, tokens):
-            nc.scalar.activation(
-                out=roots[:, t, tokens], in_=sums[:, t, tokens], func=ACT.Abs_reciprocal_sqrt, scale=0.5, bias=1.0
-            )
+        def turned_sums(t, tokens, pair, tag):
+            sums = psum.tile([P, width(tokens)], F32, name="sums%d_%d" % (t, tokens.start), tag=tag)
+            for lo in range(0, width(tokens), CHUNK):
+                own = windows[t][:, tokens.start + lo : tokens.start + lo + CHUNK]
+                for src, start in ((own, True), (pair[:, lo : lo + CHUNK], False)):
+                    nc.tensor.matmul(
+                        sums[:, lo : lo + CHUNK], lhsT=src, rhs=identity[:], start=start, stop=not start, is_transpose=True
+                    )
+            return sums
 
-        def normalise(t, tokens):
-            nc.vector.scalar_tensor_tensor(
-                out=planes[:, t, tokens],
-                in0=y_view(t, tokens),
-                scalar=gain[:, t : t + 1],
-                in1=roots[:, t, tokens],
-                op0=ALU.mult,
-                op1=ALU.mult,
-            )
+        def root(dst, sums):
+            nc.scalar.activation(out=dst, in_=sums[:], func=ACT.Abs_reciprocal_sqrt, scale=0.5, bias=1.0)
 
-        w2_grouped = held.tile([P, N * PACK], BF16, name="w2_grouped", align_bytes=64)
-        w2_codes = held.tile([P, N], U32, name="w2_codes", align_bytes=64)
+        roots = {}
+
+        def turn_back(t, c, turned):
+            if c not in roots:
+                roots[c] = psum.tile([P, PACK, CHUNK], F32, name="roots%d" % c, tag=("roots", "y0_0", "y0_256", "y1_0")[c])
+            nc.tensor.transpose(roots[c][:, t, :], turned, identity[:])
+
         w2_scales = held.tile([P, N], U8, name="w2_scales", align_bytes=64)
-
-        def group_w2(block):
-            cols = slice(P * block, P * (block + 1))
-            nc.scalar.copy(
-                out=w2_grouped[:, PACK * cols.start : PACK * cols.stop].rearrange("p (c i j) -> p c j i", i=LINE, j=PACK),
-                in_=w2_raw[:, :, cols].rearrange("p j (c i) -> p c j i", i=LINE),
-            )
 
         z = [held.tile([P, S // 2 * PACK], BF16, name="z%d" % h, align_bytes=64) for h in range(2)]
         z_codes = [held.tile([P, S // 2], U32, name="z_codes%d" % h, align_bytes=64) for h in range(2)]
@@ -195,11 +196,13 @@ def tile_picked_lrn8_none_p_kernel(tc, x_words, x_scales, w1, gn, w2, offs, p1, 
             h, lo = divmod(tokens.start, S // 2)
             return h, slice(lo, lo + width(tokens))
 
-        def group_z(tokens):
-            h, mine = within_half(tokens)
-            nc.vector.tensor_copy(
-                out=z[h][:, PACK * mine.start : PACK * mine.stop].rearrange("p (u i t) -> p u t i", i=LINE, t=PACK),
-                in_=planes[:, :, tokens].rearrange("p t (u i) -> p u t i", i=LINE),
+        def normalise(c):
+            h, mine = within_half(CHUNKS[c])
+            nc.vector.tensor_tensor(
+                z[h][:, PACK * mine.start : PACK * mine.stop].rearrange("p (u i t) -> p u t i", i=LINE, t=PACK),
+                roots[c][:].rearrange("p t (u i) -> p u t i", i=LINE),
+                gained[:, :, CHUNKS[c]].rearrange("p t (u i) -> p u t i", i=LINE),
+                ALU.mult,
             )
 
         def out_banks(h, tags):
@@ -236,51 +239,66 @@ def tile_picked_lrn8_none_p_kernel(tc, x_words, x_scales, w1, gn, w2, offs, p1, 
             rows = out[P * blocks * b : P * blocks * (b + 1), HALVES[h]]
             nc.sync.dma_start(rows.rearrange("(i p) n -> p i n", p=P), result[:])
 
-        last = PACK - 1
-        for t in range(last):
-            for part, bank in y[t]:
-                square(windows[t], t, part)
-                if t == 0:
-                    square(addend[:, 0, :], t, part)
-            if t > 0:
-                for half in HALVES:
-                    fetch(t, half)
-            for half in HALVES:
-                first_add(t, half)
-            for half in HALVES:
-                second_add(t, half)
-        square(windows[last], last, slice(0, S))
+        fetched = [held.tile([P, S], F32, name="fetched%d" % t, tag="fetched%d" % t, align_bytes=64) for t in range(last)]
+        fetched3 = [held.tile([P, S // 2], F32, name="fetched3_%d" % h, tag="fetched3_%d" % h, align_bytes=64) for h in range(2)]
+        pairs = [held.tile([P, S], F32, name="pair%d" % t) for t in range(last)]
+        pair3 = held.tile([P, S // 2], F32, name="pair3")
+        turned = [held.tile([P, S], F32, name="turned%d" % t) for t in range(last)]
+        turned3 = [held.tile([P, S // 2], F32, name="turned3_%d" % h, tag="turned3_%d" % h, align_bytes=64) for h in range(2)]
+
         for half in HALVES:
-            fetch(last, half)
-        root(0, first)
-        root(1, first)
-        group_w2(0)
-        group_w2(1)
-        first_add(last, first)
-        normalise(0, first)
-        second_add(last, first)
-        first_add(last, later)
-        root(2, first)
-        root(last, first)
-        group_w2(2)
-        group_w2(3)
-        for t in range(1, PACK):
-            normalise(t, first)
-        second_add(last, later)
-        group_z(first)
-        for t in range(PACK):
-            root(t, later)
+            square(0, half)
+        for half in HALVES:
+            fetch_vector(fetched[0][:, half], 0, half)
+        for half in HALVES:
+            add_second(pairs[0][:, half], 0, half, fetched[0][:, half])
+        square(1, everyone)
+        square(2, everyone)
+        fetch_scalar(fetched[1][:], 1, everyone)
+        add_second(pairs[1][:], 1, everyone, fetched[1][:])
+        square(last, everyone)
+        fetch_vector(fetched3[1][:], last, later)
+        fetch_scalar(fetched[2][:], 2, everyone)
+        add_second(pairs[2][:], 2, everyone, fetched[2][:])
+        fetch_scalar(fetched3[0][:], last, first)
+        add_second(pair3[:], last, first, fetched3[0][:])
+        pair3_later = held.tile([P, S // 2], F32, name="pair3_later", tag="fetched2", align_bytes=64)
+        add_second(pair3_later[:], last, later, fetched3[1][:])
+        w2_grouped = held.tile([P, N * PACK], BF16, name="w2_grouped", tag="fetched3_0", align_bytes=64)
+        nc.vector.tensor_copy(
+            out=w2_grouped[:].rearrange("p (c i j) -> p c j i", i=LINE, j=PACK),
+            in_=w2_raw[:].rearrange("p j (c i) -> p c j i", i=LINE),
+        )
+
+        for t in range(last):
+            root(turned[t][:], turned_sums(t, everyone, pairs[t], "sums%d" % (t % 2)))
+            gain_y(t, first)
+            for c in range(2):
+                turn_back(t, c, turned[t][:, CHUNKS[c]])
+        root(turned3[0][:], turned_sums(last, first, pair3, "sums1"))
+        gain_y(last, first)
+        for c in range(2):
+            turn_back(last, c, turned3[0][:, CHUNKS[c]])
+        normalise(0)
+        normalise(1)
+        w2_codes = held.tile([P, N], U32, name="w2_codes", tag="turned3_0", align_bytes=64)
         nc.vector.quantize_mx(out=w2_codes[:].bitcast(FP8X4), scales=w2_scales[:], in_=w2_grouped[:])
-        quantise_z(first)
-        banks = out_banks(0, ("out0", "out1"))
-        second_layer(first, banks, range(N // P))
         for t in range(PACK):
-            normalise(t, later)
+            gain_y(t, later)
+        for t in range(last):
+            for c in range(2, 4):
+                turn_back(t, c, turned[t][:, CHUNKS[c]])
+        root(turned3[1][:], turned_sums(last, later, pair3_later, "sums0"))
+        for c in range(2):
+            turn_back(last, 2 + c, turned3[1][:, CHUNKS[c]])
+        quantise_z(first)
+        banks = out_banks(0, ("y2_0", "y3_0"))
+        second_layer(first, banks, range(N // P))
         for b in range(len(banks)):
             store(0, banks, b, nc.scalar.copy)
-        for piece in CHUNKS[2:]:
-            group_z(piece)
-        banks = out_banks(1, ("out2", "y0_0", "y0_256", "y1_0"))
+        normalise(2)
+        normalise(3)
+        banks = out_banks(1, ("roots", "y0_0", "sums0", "sums1"))
         for piece in CHUNKS[2:]:
             quantise_z(piece)
             second_layer(piece, banks, (0, 1))

@@ -54,9 +54,7 @@ def tile_picked_lrn8_none_p_kernel(tc, x_words, x_scales, w1, gn, w2, offs, p1, 
         nc.gpsimd.memset(warm[:, 0:1], 1.0)
         nc.scalar.activation(out=warm[:, 1:2], in_=warm[:, 0:1], func=ACT.Abs_reciprocal_sqrt, scale=0.5, bias=1.0)
 
-        windows = [held.tile([P, 2 * S if t in (1, 2) else S], F32, name="window%d" % t) for t in range(PACK)]
-        for t in (1, 2):
-            nc.gpsimd.memset(windows[t][:, S : 2 * S], 0.0)
+        windows = [held.tile([P, S], F32, name="window%d" % t) for t in range(PACK)]
         identity = held.tile([P, P], F32, name="identity")
         make_identity(nc, identity[:])
 
@@ -166,15 +164,17 @@ def tile_picked_lrn8_none_p_kernel(tc, x_words, x_scales, w1, gn, w2, offs, p1, 
         def add_second(dst, t, tokens, fetched):
             nc.vector.tensor_tensor(dst, look_up(t, 1, tokens), fetched, ALU.add)
 
-        def turned_sums(t, tokens, pair, tag):
-            sums = psum.tile([P, width(tokens)], F32, name="sums%d_%d" % (t, tokens.start), tag=tag)
-            for lo in range(0, width(tokens), CHUNK):
-                own = windows[t][:, tokens.start + lo : tokens.start + lo + CHUNK]
-                for src, start in ((own, True), (pair[:, lo : lo + CHUNK], False)):
-                    nc.tensor.matmul(
-                        sums[:, lo : lo + CHUNK], lhsT=src, rhs=identity[:], start=start, stop=not start, is_transpose=True
-                    )
-            return sums
+        def add_turned(sums, tiles, tokens, terms, start, stop):
+            blocks = [(i, t, lo) for i, t in enumerate(tiles) for lo in range(0, width(tokens), CHUNK)]
+            for n, (i, t, lo) in enumerate(blocks):
+                nc.tensor.matmul(
+                    sums[:, i, lo : lo + CHUNK],
+                    lhsT=terms[t][:, tokens.start + lo : tokens.start + lo + CHUNK],
+                    rhs=identity[:],
+                    start=start and n == 0,
+                    stop=stop and n == len(blocks) - 1,
+                    is_transpose=True,
+                )
 
         def root(dst, sums):
             nc.scalar.activation(out=dst, in_=sums[:], func=ACT.Abs_reciprocal_sqrt, scale=0.5, bias=1.0)
@@ -183,7 +183,7 @@ def tile_picked_lrn8_none_p_kernel(tc, x_words, x_scales, w1, gn, w2, offs, p1, 
 
         def turn_back(t, c, turned):
             if c not in roots:
-                roots[c] = psum.tile([P, PACK, CHUNK], F32, name="roots%d" % c, tag=("roots", "y0_0", "y0_256", "y1_0")[c])
+                roots[c] = psum.tile([P, PACK, CHUNK], F32, name="roots%d" % c, tag=("y0_0", "sums0", "sums1", "sums2")[c])
             nc.tensor.transpose(roots[c][:, t, :], turned, identity[:])
 
         w2_scales = held.tile([P, N], U8, name="w2_scales", align_bytes=64)
@@ -239,66 +239,72 @@ def tile_picked_lrn8_none_p_kernel(tc, x_words, x_scales, w1, gn, w2, offs, p1, 
             rows = out[P * blocks * b : P * blocks * (b + 1), HALVES[h]]
             nc.sync.dma_start(rows.rearrange("(i p) n -> p i n", p=P), result[:])
 
-        fetched = [held.tile([P, S], F32, name="fetched%d" % t, tag="fetched%d" % t, align_bytes=64) for t in range(last)]
-        fetched3 = [held.tile([P, S // 2], F32, name="fetched3_%d" % h, tag="fetched3_%d" % h, align_bytes=64) for h in range(2)]
-        pairs = [held.tile([P, S], F32, name="pair%d" % t) for t in range(last)]
-        pair3 = held.tile([P, S // 2], F32, name="pair3")
-        turned = [held.tile([P, S], F32, name="turned%d" % t) for t in range(last)]
-        turned3 = [held.tile([P, S // 2], F32, name="turned3_%d" % h, tag="turned3_%d" % h, align_bytes=64) for h in range(2)]
+        fetched = [
+            [held.tile([P, S // 2], F32, name="fetched%d_%d" % (t, h), tag="fetched%d_%d" % (t, h), align_bytes=64) for h in range(2)]
+            for t in range(PACK)
+        ]
+        pairs = [held.tile([P, S], F32, name="pair%d" % t) for t in range(PACK)]
+        turned = held.tile([P, PACK, S], F32, name="turned")
+        couples = ((0, 1), (2, 3))
+
+        def roots_of(h, k):
+            sums = psum.tile([P, 2, S // 2], F32, name="sums%d_%d" % (h, k), tag=(("sums0", "sums1"), ("sums2", "y0_256"))[h][k])
+            add_turned(sums, couples[k], HALVES[h], windows, True, False)
+            add_turned(sums, couples[k], HALVES[h], pairs, False, True)
+            root(turned[:, 2 * k : 2 * k + 2, HALVES[h]], sums)
+
+        def roots_back(h, k):
+            for t in couples[k]:
+                for c in (2 * h, 2 * h + 1):
+                    turn_back(t, c, turned[:, t, CHUNKS[c]])
 
         for half in HALVES:
             square(0, half)
-        for half in HALVES:
-            fetch_vector(fetched[0][:, half], 0, half)
-        for half in HALVES:
-            add_second(pairs[0][:, half], 0, half, fetched[0][:, half])
+        for h, half in enumerate(HALVES):
+            fetch_vector(fetched[0][h][:], 0, half)
+        for h, half in enumerate(HALVES):
+            add_second(pairs[0][:, half], 0, half, fetched[0][h][:])
         square(1, everyone)
         square(2, everyone)
-        fetch_scalar(fetched[1][:], 1, everyone)
-        add_second(pairs[1][:], 1, everyone, fetched[1][:])
-        square(last, everyone)
-        fetch_vector(fetched3[1][:], last, later)
-        fetch_scalar(fetched[2][:], 2, everyone)
-        add_second(pairs[2][:], 2, everyone, fetched[2][:])
-        fetch_scalar(fetched3[0][:], last, first)
-        add_second(pair3[:], last, first, fetched3[0][:])
-        pair3_later = held.tile([P, S // 2], F32, name="pair3_later", tag="fetched2", align_bytes=64)
-        add_second(pair3_later[:], last, later, fetched3[1][:])
-        w2_grouped = held.tile([P, N * PACK], BF16, name="w2_grouped", tag="fetched3_0", align_bytes=64)
+        for h, half in enumerate(HALVES):
+            for t in range(1, PACK):
+                fetch_scalar(fetched[t][h][:], t, half)
+                add_second(pairs[t][:, half], t, half, fetched[t][h][:])
+                if (h, t) == (0, 1):
+                    square(last, everyone)
+        w2_grouped = held.tile([P, N * PACK], BF16, name="w2_grouped", tag="fetched2_1", align_bytes=64)
         nc.vector.tensor_copy(
             out=w2_grouped[:].rearrange("p (c i j) -> p c j i", i=LINE, j=PACK),
             in_=w2_raw[:].rearrange("p j (c i) -> p c j i", i=LINE),
         )
+        w2_codes = held.tile([P, N], U32, name="w2_codes", align_bytes=64)
+        nc.vector.quantize_mx(out=w2_codes[:].bitcast(FP8X4), scales=w2_scales[:], in_=w2_grouped[:])
 
-        for t in range(last):
-            root(turned[t][:], turned_sums(t, everyone, pairs[t], "sums%d" % (t % 2)))
+        for half in HALVES:
+            gain_y(0, half)
+        for k in range(2):
+            roots_of(0, k)
+        for t in range(1, PACK):
             gain_y(t, first)
-            for c in range(2):
-                turn_back(t, c, turned[t][:, CHUNKS[c]])
-        root(turned3[0][:], turned_sums(last, first, pair3, "sums1"))
-        gain_y(last, first)
-        for c in range(2):
-            turn_back(last, c, turned3[0][:, CHUNKS[c]])
+        for k in range(2):
+            roots_back(0, k)
         normalise(0)
         normalise(1)
-        w2_codes = held.tile([P, N], U32, name="w2_codes", tag="turned3_0", align_bytes=64)
-        nc.vector.quantize_mx(out=w2_codes[:].bitcast(FP8X4), scales=w2_scales[:], in_=w2_grouped[:])
-        for t in range(PACK):
+        for k in range(2):
+            roots_of(1, k)
+        for t in range(1, PACK):
             gain_y(t, later)
-        for t in range(last):
-            for c in range(2, 4):
-                turn_back(t, c, turned[t][:, CHUNKS[c]])
-        root(turned3[1][:], turned_sums(last, later, pair3_later, "sums0"))
-        for c in range(2):
-            turn_back(last, 2 + c, turned3[1][:, CHUNKS[c]])
-        quantise_z(first)
-        banks = out_banks(0, ("y2_0", "y3_0"))
+        for k in range(2):
+            roots_back(1, k)
+        for piece in CHUNKS[:2]:
+            quantise_z(piece)
+        banks = out_banks(0, ("y0_0", "sums0"))
         second_layer(first, banks, range(N // P))
         for b in range(len(banks)):
             store(0, banks, b, nc.scalar.copy)
         normalise(2)
         normalise(3)
-        banks = out_banks(1, ("roots", "y0_0", "sums0", "sums1"))
+        banks = out_banks(1, ("y1_0", "y2_0", "y3_0", "y0_256"))
         for piece in CHUNKS[2:]:
             quantise_z(piece)
             second_layer(piece, banks, (0, 1))

@@ -54,7 +54,8 @@ def tile_picked_lrn8_none_p_kernel(tc, x_words, x_scales, w1, gn, w2, offs, p1, 
         nc.gpsimd.memset(warm[:, 0:1], 1.0)
         nc.scalar.activation(out=warm[:, 1:2], in_=warm[:, 0:1], func=ACT.Abs_reciprocal_sqrt, scale=0.5, bias=1.0)
 
-        windows = [held.tile([P, S], F32, name="window%d" % t) for t in range(PACK)]
+        windows = [held.tile([P, 2 * S if t == 0 else S], F32, name="window%d" % t) for t in range(PACK)]
+        nc.gpsimd.memset(windows[0][:, S : 2 * S], 0.0)
         identity = held.tile([P, P], F32, name="identity")
         make_identity(nc, identity[:])
 
@@ -85,8 +86,9 @@ def tile_picked_lrn8_none_p_kernel(tc, x_words, x_scales, w1, gn, w2, offs, p1, 
         nc.sync.dma_start(places[1][:], p2)
         gain = held.tile([P, PACK], F32, name="gain")
         nc.sync.dma_start(gain[:], gn.rearrange("(p t) o -> p (t o)", t=PACK))
-        w2_raw = held.tile([P, PACK, N], F32, name="w2_raw")
-        nc.sync.dma_start(w2_raw[:], w2.rearrange("(p j) c -> p j c", j=PACK))
+        w2_raw = [held.tile([P, PACK, N // 2], F32, name="w2_raw%d" % h) for h in range(2)]
+        for h in range(2):
+            nc.sync.dma_start(w2_raw[h][:], w2[:, N // 2 * h : N // 2 * (h + 1)].rearrange("(p j) c -> p j c", j=PACK))
 
         w1_codes = [held.tile([P, H], U32, name="w1_codes%d" % g, align_bytes=64) for g in range(PASSES)]
         w1_scales = [held.tile([P, H], U8, name="w1_scales%d" % g, align_bytes=64) for g in range(PASSES)]
@@ -144,13 +146,14 @@ def tile_picked_lrn8_none_p_kernel(tc, x_words, x_scales, w1, gn, w2, offs, p1, 
         first, later = HALVES
         everyone = slice(0, S)
         last = PACK - 1
-        gained = held.tile([P, PACK, S], F32, name="gained")
+        gained = [held.tile([P, PACK, S // 2], F32, name="gained%d" % h) for h in range(2)]
 
         def square(t, tokens):
             nc.scalar.activation(out=windows[t][:, tokens], in_=y_view(t, tokens), func=ACT.Square)
 
         def gain_y(t, tokens):
-            nc.scalar.activation(out=gained[:, t, tokens], in_=y_view(t, tokens), func=ACT.Copy, scale=gain[:, t : t + 1])
+            dst = gained[tokens.start // (S // 2)][:, t, :]
+            nc.scalar.activation(out=dst, in_=y_view(t, tokens), func=ACT.Copy, scale=gain[:, t : t + 1])
 
         def look_up(t, a, tokens):
             return windows[t][:].indirect(places[a][:, list_columns(tokens)])
@@ -158,21 +161,21 @@ def tile_picked_lrn8_none_p_kernel(tc, x_words, x_scales, w1, gn, w2, offs, p1, 
         def fetch_scalar(dst, t, tokens):
             nc.scalar.activation(out=dst, in_=look_up(t, 0, tokens), func=ACT.Copy)
 
-        def fetch_vector(dst, t, tokens):
-            nc.vector.tensor_copy(dst, look_up(t, 0, tokens))
+        def fetch_vector(dst, t, a, tokens):
+            nc.vector.tensor_copy(dst, look_up(t, a, tokens))
 
         def add_second(dst, t, tokens, fetched):
             nc.vector.tensor_tensor(dst, look_up(t, 1, tokens), fetched, ALU.add)
 
-        def add_turned(sums, tiles, tokens, terms, start, stop):
-            blocks = [(i, t, lo) for i, t in enumerate(tiles) for lo in range(0, width(tokens), CHUNK)]
-            for n, (i, t, lo) in enumerate(blocks):
+        def add_turned(sums, terms):
+            blocks = [(i, term, lo) for i, term in terms for lo in range(0, S // 2, CHUNK)]
+            for n, (i, term, lo) in enumerate(blocks):
                 nc.tensor.matmul(
                     sums[:, i, lo : lo + CHUNK],
-                    lhsT=terms[t][:, tokens.start + lo : tokens.start + lo + CHUNK],
+                    lhsT=term[:, lo : lo + CHUNK],
                     rhs=identity[:],
-                    start=start and n == 0,
-                    stop=stop and n == len(blocks) - 1,
+                    start=n == 0,
+                    stop=n == len(blocks) - 1,
                     is_transpose=True,
                 )
 
@@ -183,7 +186,7 @@ def tile_picked_lrn8_none_p_kernel(tc, x_words, x_scales, w1, gn, w2, offs, p1, 
 
         def turn_back(t, c, turned):
             if c not in roots:
-                roots[c] = psum.tile([P, PACK, CHUNK], F32, name="roots%d" % c, tag=("y0_0", "sums0", "sums1", "sums2")[c])
+                roots[c] = psum.tile([P, PACK, CHUNK], F32, name="roots%d" % c, tag=("sums0", "y0_0", "sums2", "sums0")[c])
             nc.tensor.transpose(roots[c][:, t, :], turned, identity[:])
 
         w2_scales = held.tile([P, N], U8, name="w2_scales", align_bytes=64)
@@ -201,7 +204,7 @@ def tile_picked_lrn8_none_p_kernel(tc, x_words, x_scales, w1, gn, w2, offs, p1, 
             nc.vector.tensor_tensor(
                 z[h][:, PACK * mine.start : PACK * mine.stop].rearrange("p (u i t) -> p u t i", i=LINE, t=PACK),
                 roots[c][:].rearrange("p t (u i) -> p u t i", i=LINE),
-                gained[:, :, CHUNKS[c]].rearrange("p t (u i) -> p u t i", i=LINE),
+                gained[h][:, :, mine].rearrange("p t (u i) -> p u t i", i=LINE),
                 ALU.mult,
             )
 
@@ -239,72 +242,90 @@ def tile_picked_lrn8_none_p_kernel(tc, x_words, x_scales, w1, gn, w2, offs, p1, 
             rows = out[P * blocks * b : P * blocks * (b + 1), HALVES[h]]
             nc.sync.dma_start(rows.rearrange("(i p) n -> p i n", p=P), result[:])
 
-        fetched = [
-            [held.tile([P, S // 2], F32, name="fetched%d_%d" % (t, h), tag="fetched%d_%d" % (t, h), align_bytes=64) for h in range(2)]
-            for t in range(PACK)
-        ]
-        pairs = [held.tile([P, S], F32, name="pair%d" % t) for t in range(PACK)]
-        turned = held.tile([P, PACK, S], F32, name="turned")
+        fetched = [held.tile([P, S], F32, name="fetched%d" % t, tag="fetched%d" % t, align_bytes=64) for t in range(PACK)]
+        fetched2_first = held.tile([P, S // 2], F32, name="fetched2_first", tag="fetched2_first")
+        pairs = {(h, t): held.tile([P, S // 2], F32, name="pair%d_%d" % (h, t))[:] for t in range(1, PACK) for h in range(2) if (h, t) != (1, last)}
+        pair0 = held.tile([P, S], F32, name="pair0")
+        for h, half in enumerate(HALVES):
+            pairs[h, 0] = pair0[:, half]
+        turned = [held.tile([P, PACK, S // 2], F32, name="turned%d" % h) for h in range(2)]
         couples = ((0, 1), (2, 3))
+        unfused = ((0, 0), (1, 0), (0, 1))
 
         def roots_of(h, k):
-            sums = psum.tile([P, 2, S // 2], F32, name="sums%d_%d" % (h, k), tag=(("sums0", "sums1"), ("sums2", "y0_256"))[h][k])
-            add_turned(sums, couples[k], HALVES[h], windows, True, False)
-            add_turned(sums, couples[k], HALVES[h], pairs, False, True)
-            root(turned[:, 2 * k : 2 * k + 2, HALVES[h]], sums)
+            sums = psum.tile([P, 2, S // 2], F32, name="sums%d_%d" % (h, k), tag=(("sums0", "sums1"), ("sums2", "sums1"))[h][k])
+            terms = [(i, windows[t][:, HALVES[h]]) for i, t in enumerate(couples[k])]
+            terms += [(i, fetched[t][:, HALVES[h]]) for i, t in enumerate(couples[k]) if (h, t) in unfused]
+            terms += [(i, pairs[h, t]) for i, t in enumerate(couples[k])]
+            add_turned(sums, terms)
+            root(turned[h][:, 2 * k : 2 * k + 2, :], sums)
 
         def roots_back(h, k):
-            for t in couples[k]:
-                for c in (2 * h, 2 * h + 1):
-                    turn_back(t, c, turned[:, t, CHUNKS[c]])
+            for c in (2 * h, 2 * h + 1):
+                for t in couples[k]:
+                    turn_back(t, c, turned[h][:, t, CHUNKS[c % 2]])
 
         for half in HALVES:
             square(0, half)
-        for h, half in enumerate(HALVES):
-            fetch_vector(fetched[0][h][:], 0, half)
-        for h, half in enumerate(HALVES):
-            add_second(pairs[0][:, half], 0, half, fetched[0][h][:])
+        fetch_vector(fetched[0][:], 0, 0, everyone)
+        fetch_vector(pair0[:], 0, 1, everyone)
         square(1, everyone)
+        fetch_vector(pairs[0, 1], 1, 1, first)
         square(2, everyone)
-        for h, half in enumerate(HALVES):
-            for t in range(1, PACK):
-                fetch_scalar(fetched[t][h][:], t, half)
-                add_second(pairs[t][:, half], t, half, fetched[t][h][:])
-                if (h, t) == (0, 1):
-                    square(last, everyone)
-        w2_grouped = held.tile([P, N * PACK], BF16, name="w2_grouped", tag="fetched2_1", align_bytes=64)
-        nc.vector.tensor_copy(
-            out=w2_grouped[:].rearrange("p (c i j) -> p c j i", i=LINE, j=PACK),
-            in_=w2_raw[:].rearrange("p j (c i) -> p c j i", i=LINE),
-        )
-        w2_codes = held.tile([P, N], U32, name="w2_codes", align_bytes=64)
+        fetch_scalar(fetched[1][:, first], 1, first)
+        square(last, everyone)
+        fetch_vector(fetched[last][:, later], last, 0, later)
+        fetch_scalar(fetched2_first[:], 2, first)
+        add_second(pairs[0, 2], 2, first, fetched2_first[:])
+        fetch_scalar(fetched[last][:, first], last, first)
+        add_second(pairs[0, last], last, first, fetched[last][:, first])
+        fetch_scalar(fetched[1][:, later], 1, later)
+        add_second(pairs[1, 1], 1, later, fetched[1][:, later])
+        pair3_later = held.tile([P, S // 2], F32, name="pair3_later", tag="fetched2_first")
+        pairs[1, last] = pair3_later[:]
+        add_second(pairs[1, last], last, later, fetched[last][:, later])
+        gain_y(0, first)
+        roots_of(0, 0)
+        fetch_scalar(fetched[2][:, later], 2, later)
+        add_second(pairs[1, 2], 2, later, fetched[2][:, later])
+
+        w2_grouped = held.tile([P, N * PACK], BF16, name="w2_grouped", align_bytes=64)
+        for h in range(2):
+            nc.gpsimd.tensor_scalar(
+                w2_grouped[:, N * 2 * h : N * 2 * (h + 1)].rearrange("p (c j) -> p c j", j=PACK),
+                w2_raw[h][:].rearrange("p j c -> p c j"),
+                1.0,
+                0.0,
+                ALU.mult,
+                ALU.add,
+            )
+        w2_codes = held.tile([P, N], U32, name="w2_codes", tag="fetched3", align_bytes=64)
         nc.vector.quantize_mx(out=w2_codes[:].bitcast(FP8X4), scales=w2_scales[:], in_=w2_grouped[:])
 
-        for half in HALVES:
-            gain_y(0, half)
-        for k in range(2):
-            roots_of(0, k)
-        for t in range(1, PACK):
-            gain_y(t, first)
+        gain_y(1, first)
+        gain_y(2, first)
+        roots_of(0, 1)
+        gain_y(last, first)
         for k in range(2):
             roots_back(0, k)
         normalise(0)
         normalise(1)
-        for k in range(2):
-            roots_of(1, k)
+        roots_of(1, 0)
+        gain_y(0, later)
+        roots_of(1, 1)
         for t in range(1, PACK):
             gain_y(t, later)
         for k in range(2):
             roots_back(1, k)
         for piece in CHUNKS[:2]:
             quantise_z(piece)
-        banks = out_banks(0, ("y0_0", "sums0"))
+        banks = out_banks(0, ("sums1", "y3_0"))
         second_layer(first, banks, range(N // P))
         for b in range(len(banks)):
             store(0, banks, b, nc.scalar.copy)
         normalise(2)
         normalise(3)
-        banks = out_banks(1, ("y1_0", "y2_0", "y3_0", "y0_256"))
+        banks = out_banks(1, ("y0_256", "y1_0", "y2_0", "y0_0"))
         for piece in CHUNKS[2:]:
             quantise_z(piece)
             second_layer(piece, banks, (0, 1))

@@ -186,7 +186,7 @@ def tile_picked_lrn8_none_p_kernel(tc, x_words, x_scales, w1, gn, w2, offs, p1, 
 
         def turn_back(t, c, turned):
             if c not in roots:
-                roots[c] = psum.tile([P, PACK, CHUNK], F32, name="roots%d" % c, tag=("sums0", "y0_0", "sums2", "sums0")[c])
+                roots[c] = psum.tile([P, PACK, CHUNK], F32, name="roots%d" % c, tag=("sums0", "y0_256", "sums2", "y0_0")[c])
             nc.tensor.transpose(roots[c][:, t, :], turned, identity[:])
 
         w2_scales = held.tile([P, N], U8, name="w2_scales", align_bytes=64)
@@ -242,52 +242,52 @@ def tile_picked_lrn8_none_p_kernel(tc, x_words, x_scales, w1, gn, w2, offs, p1, 
             rows = out[P * blocks * b : P * blocks * (b + 1), HALVES[h]]
             nc.sync.dma_start(rows.rearrange("(i p) n -> p i n", p=P), result[:])
 
-        fetched = [held.tile([P, S], F32, name="fetched%d" % t, tag="fetched%d" % t, align_bytes=64) for t in range(PACK)]
-        fetched2_first = held.tile([P, S // 2], F32, name="fetched2_first", tag="fetched2_first")
-        pairs = {(h, t): held.tile([P, S // 2], F32, name="pair%d_%d" % (h, t))[:] for t in range(1, PACK) for h in range(2) if (h, t) != (1, last)}
-        pair0 = held.tile([P, S], F32, name="pair0")
-        for h, half in enumerate(HALVES):
-            pairs[h, 0] = pair0[:, half]
+        fetched, pairs = {}, {}
+        for name, parts in (("fetched", fetched), ("pair", pairs)):
+            whole = held.tile([P, S], F32, name="%s0" % name)
+            parts["whole"] = whole[:]
+            for h, half in enumerate(HALVES):
+                parts[h, 0] = whole[:, half]
+                for t in range(1, PACK):
+                    label = "%s%d_%d" % (name, h, t)
+                    if label != "fetched1_3":
+                        parts[h, t] = held.tile([P, S // 2], F32, name=label, tag=label, align_bytes=64)[:]
         turned = [held.tile([P, PACK, S // 2], F32, name="turned%d" % h) for h in range(2)]
-        couples = ((0, 1), (2, 3))
         unfused = ((0, 0), (1, 0), (0, 1))
 
-        def roots_of(h, k):
-            sums = psum.tile([P, 2, S // 2], F32, name="sums%d_%d" % (h, k), tag=(("sums0", "sums1"), ("sums2", "sums1"))[h][k])
-            terms = [(i, windows[t][:, HALVES[h]]) for i, t in enumerate(couples[k])]
-            terms += [(i, fetched[t][:, HALVES[h]]) for i, t in enumerate(couples[k]) if (h, t) in unfused]
-            terms += [(i, pairs[h, t]) for i, t in enumerate(couples[k])]
+        def roots_of(h, tiles, bank):
+            sums = psum.tile([P, len(tiles), S // 2], F32, name="sums%d_%d" % (h, tiles[0]), tag=bank)
+            terms = [(i, windows[t][:, HALVES[h]]) for i, t in enumerate(tiles)]
+            terms += [(i, fetched[h, t]) for i, t in enumerate(tiles) if (h, t) in unfused]
+            terms += [(i, pairs[h, t]) for i, t in enumerate(tiles)]
             add_turned(sums, terms)
-            root(turned[h][:, 2 * k : 2 * k + 2, :], sums)
+            root(turned[h][:, tiles[0] : tiles[-1] + 1, :], sums)
 
-        def roots_back(h, k):
-            for c in (2 * h, 2 * h + 1):
-                for t in couples[k]:
-                    turn_back(t, c, turned[h][:, t, CHUNKS[c % 2]])
+        def roots_back(h, tiles):
+            for c in range(2):
+                for t in tiles:
+                    turn_back(t, 2 * h + c, turned[h][:, t, CHUNKS[c]])
+
+        def look_up_both(h, t):
+            fetch_scalar(fetched[h, t], t, HALVES[h])
+            add_second(pairs[h, t], t, HALVES[h], fetched[h, t])
 
         for half in HALVES:
             square(0, half)
-        fetch_vector(fetched[0][:], 0, 0, everyone)
-        fetch_vector(pair0[:], 0, 1, everyone)
+        fetch_vector(fetched["whole"], 0, 0, everyone)
+        fetch_vector(pairs["whole"], 0, 1, everyone)
         square(1, everyone)
         fetch_vector(pairs[0, 1], 1, 1, first)
         square(2, everyone)
-        fetch_scalar(fetched[1][:, first], 1, first)
+        fetch_scalar(fetched[0, 1], 1, first)
         square(last, everyone)
-        fetch_vector(fetched[last][:, later], last, 0, later)
-        fetch_scalar(fetched2_first[:], 2, first)
-        add_second(pairs[0, 2], 2, first, fetched2_first[:])
-        fetch_scalar(fetched[last][:, first], last, first)
-        add_second(pairs[0, last], last, first, fetched[last][:, first])
-        fetch_scalar(fetched[1][:, later], 1, later)
-        add_second(pairs[1, 1], 1, later, fetched[1][:, later])
-        pair3_later = held.tile([P, S // 2], F32, name="pair3_later", tag="fetched2_first")
-        pairs[1, last] = pair3_later[:]
-        add_second(pairs[1, last], last, later, fetched[last][:, later])
-        gain_y(0, first)
-        roots_of(0, 0)
-        fetch_scalar(fetched[2][:, later], 2, later)
-        add_second(pairs[1, 2], 2, later, fetched[2][:, later])
+        look_up_both(0, 2)
+        look_up_both(0, last)
+        look_up_both(1, 1)
+        fetched[1, last] = held.tile([P, S // 2], F32, name="fetched1_3", tag="fetched0_3", align_bytes=64)[:]
+        fetch_vector(fetched[1, last], last, 0, later)
+        look_up_both(1, 2)
+        add_second(pairs[1, last], last, later, fetched[1, last])
 
         w2_grouped = held.tile([P, N * PACK], BF16, name="w2_grouped", align_bytes=64)
         for h in range(2):
@@ -299,24 +299,27 @@ def tile_picked_lrn8_none_p_kernel(tc, x_words, x_scales, w1, gn, w2, offs, p1, 
                 ALU.mult,
                 ALU.add,
             )
-        w2_codes = held.tile([P, N], U32, name="w2_codes", tag="fetched3", align_bytes=64)
+        w2_codes = held.tile([P, N], U32, name="w2_codes", tag="fetched1_2", align_bytes=64)
         nc.vector.quantize_mx(out=w2_codes[:].bitcast(FP8X4), scales=w2_scales[:], in_=w2_grouped[:])
 
-        gain_y(1, first)
-        gain_y(2, first)
-        roots_of(0, 1)
-        gain_y(last, first)
-        for k in range(2):
-            roots_back(0, k)
+        for half in HALVES:
+            gain_y(0, half)
+        roots_of(0, (0, 1), "sums0")
+        roots_of(0, (2, 3), "sums1")
+        for t in range(1, PACK):
+            gain_y(t, first)
+        roots_back(0, (0, 1))
+        roots_back(0, (2, 3))
         normalise(0)
         normalise(1)
-        roots_of(1, 0)
-        gain_y(0, later)
-        roots_of(1, 1)
-        for t in range(1, PACK):
-            gain_y(t, later)
-        for k in range(2):
-            roots_back(1, k)
+        roots_of(1, (0, 1), "sums2")
+        roots_of(1, (2,), "y0_0")
+        gain_y(1, later)
+        gain_y(2, later)
+        roots_of(1, (3,), "sums1")
+        gain_y(3, later)
+        for tiles in ((0, 1), (2,), (3,)):
+            roots_back(1, tiles)
         for piece in CHUNKS[:2]:
             quantise_z(piece)
         banks = out_banks(0, ("sums1", "y3_0"))
@@ -325,7 +328,7 @@ def tile_picked_lrn8_none_p_kernel(tc, x_words, x_scales, w1, gn, w2, offs, p1, 
             store(0, banks, b, nc.scalar.copy)
         normalise(2)
         normalise(3)
-        banks = out_banks(1, ("y0_256", "y1_0", "y2_0", "y0_0"))
+        banks = out_banks(1, ("sums0", "y0_256", "y1_0", "y2_0"))
         for piece in CHUNKS[2:]:
             quantise_z(piece)
             second_layer(piece, banks, (0, 1))

@@ -152,7 +152,8 @@ def tile_picked_lrn8_none_p_kernel(tc, x_words, x_scales, w1, gn, w2, offs, p1, 
             nc.scalar.activation(out=windows[t][:, tokens], in_=y_view(t, tokens), func=ACT.Square)
 
         def gain_y(t, tokens):
-            dst = gained[tokens.start // (S // 2)][:, t, :]
+            h, mine = within_half(tokens)
+            dst = gained[h][:, t, mine]
             nc.scalar.activation(out=dst, in_=y_view(t, tokens), func=ACT.Copy, scale=gain[:, t : t + 1])
 
         def look_up(t, a, tokens):
@@ -186,7 +187,7 @@ def tile_picked_lrn8_none_p_kernel(tc, x_words, x_scales, w1, gn, w2, offs, p1, 
 
         def turn_back(t, c, turned):
             if c not in roots:
-                roots[c] = psum.tile([P, PACK, CHUNK], F32, name="roots%d" % c, tag=("sums0", "y0_256", "sums2", "y0_0")[c])
+                roots[c] = psum.tile([P, PACK, CHUNK], F32, name="roots%d" % c, tag=("sums0", "y0_256", "sums2", "sums1")[c])
             nc.tensor.transpose(roots[c][:, t, :], turned, identity[:])
 
         w2_scales = held.tile([P, N], U8, name="w2_scales", align_bytes=64)
@@ -305,24 +306,27 @@ def tile_picked_lrn8_none_p_kernel(tc, x_words, x_scales, w1, gn, w2, offs, p1, 
         for half in HALVES:
             gain_y(0, half)
         roots_of(0, (0, 1), "sums0")
-        roots_of(0, (2, 3), "sums1")
-        for t in range(1, PACK):
-            gain_y(t, first)
-        roots_back(0, (0, 1))
-        roots_back(0, (2, 3))
+        roots_of(0, (2,), "sums1")
+        gain_y(1, first)
+        gain_y(2, first)
+        roots_of(0, (3,), "y0_0")
+        gain_y(3, first)
+        for tiles in ((0, 1), (2,), (3,)):
+            roots_back(0, tiles)
         normalise(0)
         normalise(1)
         roots_of(1, (0, 1), "sums2")
-        roots_of(1, (2,), "y0_0")
+        roots_of(1, (2,), "sums1")
         gain_y(1, later)
-        gain_y(2, later)
-        roots_of(1, (3,), "sums1")
-        gain_y(3, later)
+        roots_of(1, (3,), "y0_0")
+        for piece in CHUNKS[2:]:
+            gain_y(2, piece)
+            gain_y(3, piece)
         for tiles in ((0, 1), (2,), (3,)):
             roots_back(1, tiles)
         for piece in CHUNKS[:2]:
             quantise_z(piece)
-        banks = out_banks(0, ("sums1", "y3_0"))
+        banks = out_banks(0, ("y0_0", "y3_0"))
         second_layer(first, banks, range(N // P))
         for b in range(len(banks)):
             store(0, banks, b, nc.scalar.copy)

@@ -287,7 +287,9 @@ def tile_picked_lrn8_none_p_kernel(tc, x_words, x_scales, w1, gn, w2, offs, p1, 
         look_up_both(1, 1)
         fetched[1, last] = held.tile([P, S // 2], F32, name="fetched1_3", tag="fetched0_3", align_bytes=64)[:]
         fetch_vector(fetched[1, last], last, 0, later)
-        look_up_both(1, 2)
+        fetch_vector(fetched[1, 2][:, CHUNKS[1]], 2, 0, CHUNKS[3])
+        fetch_scalar(fetched[1, 2][:, CHUNKS[0]], 2, CHUNKS[2])
+        add_second(pairs[1, 2], 2, later, fetched[1, 2])
         add_second(pairs[1, last], last, later, fetched[1, last])
 
         w2_grouped = held.tile([P, N * PACK], BF16, name="w2_grouped", align_bytes=64)
@@ -319,9 +321,8 @@ def tile_picked_lrn8_none_p_kernel(tc, x_words, x_scales, w1, gn, w2, offs, p1, 
         roots_of(1, (2,), "sums1")
         gain_y(1, later)
         roots_of(1, (3,), "y0_0")
-        for piece in CHUNKS[2:]:
-            gain_y(2, piece)
-            gain_y(3, piece)
+        gain_y(2, later)
+        gain_y(3, later)
         for tiles in ((0, 1), (2,), (3,)):
             roots_back(1, tiles)
         for piece in CHUNKS[:2]:

from contextlib import ExitStack

import concourse.mybir as mybir
from concourse.masks import make_identity

K, T, S, N, H = 1024, 2048, 512, 512, 512
FLOPS = 2 * K * H * S + 2 * H * N * S

F32 = mybir.dt.float32
BF16 = mybir.dt.bfloat16
I32 = mybir.dt.int32
U32 = mybir.dt.uint32
U16 = mybir.dt.uint16
U8 = mybir.dt.uint8
FP8X4 = mybir.dt.float8_e4m3fn_x4
ACT = mybir.ActivationFunctionType
ALU = mybir.AluOpType

P = 128
PACK = 4
K_PASS = P * PACK
PASSES = K // K_PASS
LIST_COLUMN = 16
QUADRANT = 32
SCALE_ROWS = 4
LINE = 4
HALVES = (slice(0, S // 2), slice(S // 2, S))
CHUNK = 128
CHUNKS = tuple(slice(a, a + CHUNK) for a in range(0, S, CHUNK))
SCALAR_GROUPS = 48


def width(tokens):
    return tokens.stop - tokens.start


def list_columns(tokens):
    return slice(tokens.start // LIST_COLUMN, tokens.stop // LIST_COLUMN)


def tile_picked_lrn8_none_p_kernel(tc, x_words, x_scales, w1, gn, w2, offs, p1, p2, out):
    nc = tc.nc
    with ExitStack() as ctx:
        held = ctx.enter_context(tc.tile_pool(name="held", bufs=1))
        psum = ctx.enter_context(tc.psum_pool(name="psum", bufs=1))

        picked = held.tile([P, S // LIST_COLUMN], U16, name="picked")
        places = [held.tile([P, S // LIST_COLUMN], U16, name="places%d" % a) for a in range(2)]

        scale_table = held.tile([P, T], U8, name="scale_table")
        nc.gpsimd.memset(scale_table[:].bitcast(I32), 0)

        warm = held.tile([P, 2], F32, name="warm")
        nc.gpsimd.memset(warm[:, 0:1], 1.0)
        nc.scalar.activation(out=warm[:, 1:2], in_=warm[:, 0:1], func=ACT.Abs_reciprocal_sqrt, scale=0.5, bias=1.0)

        windows = [held.tile([P, 2 * S if t == 0 else S], F32, name="window%d" % t) for t in range(PACK)]
        nc.gpsimd.memset(windows[0][:, S : 2 * S], 0.0)
        identity = held.tile([P, P], F32, name="identity")
        make_identity(nc, identity[:])

        w1_raw = [held.tile([P, PACK, H], F32, name="w1_raw%d" % g) for g in range(PASSES)]
        word_table = [held.tile([P, T], I32, name="word_table%d" % g) for g in range(PASSES)]

        def load_w1(g):
            nc.sync.dma_start(w1_raw[g][:], w1[K_PASS * g : K_PASS * (g + 1), :].rearrange("(p j) c -> p j c", j=PACK))

        def load_words(g):
            nc.sync.dma_start(word_table[g][:], x_words[g].rearrange("p n j -> p (n j)").bitcast(I32))

        def load_scale_rows(g):
            for r in range(SCALE_ROWS):
                nc.sync.dma_start(
                    scale_table[SCALE_ROWS * g + r : P : QUADRANT, :].bitcast(I32),
                    x_scales[g, r : SCALE_ROWS * P // QUADRANT : SCALE_ROWS, :].bitcast(I32),
                )

        load_w1(0)
        load_scale_rows(0)
        nc.sync.dma_start(picked[:], offs)
        load_words(0)
        load_scale_rows(1)
        load_w1(1)
        load_words(1)
        nc.sync.dma_start(places[0][:], p1)
        nc.sync.dma_start(places[1][:], p2)
        gain = held.tile([P, PACK], F32, name="gain")
        nc.sync.dma_start(gain[:], gn.rearrange("(p t) o -> p (t o)", t=PACK))
        w2_raw = [held.tile([P, PACK, N // 2], F32, name="w2_raw%d" % h) for h in range(2)]
        for h in range(2):
            nc.sync.dma_start(w2_raw[h][:], w2[:, N // 2 * h : N // 2 * (h + 1)].rearrange("(p j) c -> p j c", j=PACK))

        w1_codes = [held.tile([P, H], U32, name="w1_codes%d" % g, align_bytes=64) for g in range(PASSES)]
        w1_scales = [held.tile([P, H], U8, name="w1_scales%d" % g, align_bytes=64) for g in range(PASSES)]

        def quantise_w1(g):
            w1_grouped = held.tile([P, H * PACK], BF16, name="w1_grouped%d" % g, align_bytes=64)
            dst = w1_grouped[:].rearrange("p (t m j) -> p m j t", t=PACK, j=PACK)
            src = w1_raw[g][:].rearrange("p j (m t) -> p m j t", t=PACK)
            nc.scalar.copy(out=dst[:, 0:SCALAR_GROUPS], in_=src[:, 0:SCALAR_GROUPS])
            nc.vector.tensor_copy(out=dst[:, SCALAR_GROUPS:P], in_=src[:, SCALAR_GROUPS:P])
            nc.vector.quantize_mx(out=w1_codes[g][:].bitcast(FP8X4), scales=w1_scales[g][:], in_=w1_grouped[:])

        y = []
        for t in range(PACK):
            parts = HALVES if t == 0 else (slice(0, S),)
            names = ["y%d_%d" % (t, part.start) for part in parts]
            y.append([(part, psum.tile([P, width(part)], F32, name=nm, tag=nm)) for part, nm in zip(parts, names)])

        def y_view(t, tokens):
            part, bank = [entry for entry in y[t] if entry[0].start <= tokens.start < entry[0].stop][0]
            return bank[:, tokens.start - part.start : tokens.stop - part.start]

        x_scale = held.tile([P, S], U8, name="x_scale", align_bytes=64)
        x_codes = [held.tile([P, S], U32, name="x_codes%d" % g, align_bytes=64) for g in range(PASSES)]

        def gather_words(g, tokens):
            nc.vector.tensor_copy(
                x_codes[g][:, tokens], word_table[g][:].bitcast(U32).indirect(picked[:, list_columns(tokens)])
            )

        def first_layer(t, g):
            cols = slice(P * t, P * (t + 1))
            for part, bank in y[t]:
                nc.tensor.matmul_mx(
                    out=bank[:],
                    lhsT=w1_codes[g][:, cols].bitcast(FP8X4),
                    lhsT_scale=w1_scales[g][:, cols],
                    rhs=x_codes[g][:, part].bitcast(FP8X4),
                    rhs_scale=x_scale[SCALE_ROWS * g : P, part],
                    start=g == 0,
                    stop=g == PASSES - 1,
                )

        quantise_w1(0)
        gather_words(0, slice(0, S))
        nc.vector.tensor_copy(x_scale[:], scale_table[:].indirect(picked[:]))
        for t in range(PACK):
            first_layer(t, 0)
        quantise_w1(1)
        for half in HALVES:
            gather_words(1, half)
        for t in range(PACK):
            first_layer(t, 1)

        first, later = HALVES
        everyone = slice(0, S)
        last = PACK - 1
        gained = [held.tile([P, PACK, S // 2], F32, name="gained%d" % h) for h in range(2)]

        def square(t, tokens):
            nc.scalar.activation(out=windows[t][:, tokens], in_=y_view(t, tokens), func=ACT.Square)

        def gain_y(t, tokens):
            h, mine = within_half(tokens)
            dst = gained[h][:, t, mine]
            nc.scalar.activation(out=dst, in_=y_view(t, tokens), func=ACT.Copy, scale=gain[:, t : t + 1])

        def look_up(t, a, tokens):
            return windows[t][:].indirect(places[a][:, list_columns(tokens)])

        def fetch_scalar(dst, t, tokens):
            nc.scalar.activation(out=dst, in_=look_up(t, 0, tokens), func=ACT.Copy)

        def fetch_vector(dst, t, a, tokens):
            nc.vector.tensor_copy(dst, look_up(t, a, tokens))

        def add_second(dst, t, tokens, fetched):
            nc.vector.tensor_tensor(dst, look_up(t, 1, tokens), fetched, ALU.add)

        def add_turned(sums, terms):
            blocks = [(i, term, lo) for i, term in terms for lo in range(0, S // 2, CHUNK)]
            for n, (i, term, lo) in enumerate(blocks):
                nc.tensor.matmul(
                    sums[:, i, lo : lo + CHUNK],
                    lhsT=term[:, lo : lo + CHUNK],
                    rhs=identity[:],
                    start=n == 0,
                    stop=n == len(blocks) - 1,
                    is_transpose=True,
                )

        def root(dst, sums):
            nc.scalar.activation(out=dst, in_=sums[:], func=ACT.Abs_reciprocal_sqrt, scale=0.5, bias=1.0)

        roots = {}

        def turn_back(t, c, turned):
            if c not in roots:
                roots[c] = psum.tile([P, PACK, CHUNK], F32, name="roots%d" % c, tag=("sums0", "y0_256", "sums2", "sums1")[c])
            nc.tensor.transpose(roots[c][:, t, :], turned, identity[:])

        w2_scales = held.tile([P, N], U8, name="w2_scales", align_bytes=64)

        z = [held.tile([P, S // 2 * PACK], BF16, name="z%d" % h, align_bytes=64) for h in range(2)]
        z_codes = [held.tile([P, S // 2], U32, name="z_codes%d" % h, align_bytes=64) for h in range(2)]
        z_scales = [held.tile([P, S // 2], U8, name="z_scales%d" % h, align_bytes=64) for h in range(2)]

        def within_half(tokens):
            h, lo = divmod(tokens.start, S // 2)
            return h, slice(lo, lo + width(tokens))

        def normalise(c):
            h, mine = within_half(CHUNKS[c])
            nc.vector.tensor_tensor(
                z[h][:, PACK * mine.start : PACK * mine.stop].rearrange("p (u i t) -> p u t i", i=LINE, t=PACK),
                roots[c][:].rearrange("p t (u i) -> p u t i", i=LINE),
                gained[h][:, :, mine].rearrange("p t (u i) -> p u t i", i=LINE),
                ALU.mult,
            )

        def out_banks(h, tags):
            shape = [P, N // P // len(tags), S // 2]
            return [psum.tile(shape, F32, name="out%d_%d" % (h, b), tag=tag) for b, tag in enumerate(tags)]

        def quantise_z(tokens):
            h, mine = within_half(tokens)
            nc.vector.quantize_mx(
                out=z_codes[h][:, mine].bitcast(FP8X4),
                scales=z_scales[h][:, mine],
                in_=z[h][:, PACK * mine.start : PACK * mine.stop],
            )

        def second_layer(tokens, banks, blocks):
            h, mine = within_half(tokens)
            for block in blocks:
                b, i = divmod(block, N // P // len(banks))
                cols = slice(P * block, P * (block + 1))
                nc.tensor.matmul_mx(
                    out=banks[b][:, i, mine],
                    lhsT=w2_codes[:, cols].bitcast(FP8X4),
                    lhsT_scale=w2_scales[:, cols],
                    rhs=z_codes[h][:, mine].bitcast(FP8X4),
                    rhs_scale=z_scales[h][:, mine],
                    start=True,
                    stop=True,
                )

        def store(h, banks, b, copy):
            blocks = N // P // len(banks)
            result = held.tile([P, blocks, S // 2], F32, name="result%d_%d" % (h, b))
            copy(out=result[:], in_=banks[b][:])
            rows = out[P * blocks * b : P * blocks * (b + 1), HALVES[h]]
            nc.sync.dma_start(rows.rearrange("(i p) n -> p i n", p=P), result[:])

        fetched, pairs = {}, {}
        for name, parts in (("fetched", fetched), ("pair", pairs)):
            whole = held.tile([P, S], F32, name="%s0" % name)
            parts["whole"] = whole[:]
            for h, half in enumerate(HALVES):
                parts[h, 0] = whole[:, half]
                for t in range(1, PACK):
                    label = "%s%d_%d" % (name, h, t)
                    if label != "fetched1_3":
                        parts[h, t] = held.tile([P, S // 2], F32, name=label, tag=label, align_bytes=64)[:]
        turned = [held.tile([P, PACK, S // 2], F32, name="turned%d" % h) for h in range(2)]
        unfused = ((0, 0), (1, 0), (0, 1))

        def roots_of(h, tiles, bank):
            sums = psum.tile([P, len(tiles), S // 2], F32, name="sums%d_%d" % (h, tiles[0]), tag=bank)
            terms = [(i, windows[t][:, HALVES[h]]) for i, t in enumerate(tiles)]
            terms += [(i, fetched[h, t]) for i, t in enumerate(tiles) if (h, t) in unfused]
            terms += [(i, pairs[h, t]) for i, t in enumerate(tiles)]
            add_turned(sums, terms)
            root(turned[h][:, tiles[0] : tiles[-1] + 1, :], sums)

        def roots_back(h, tiles):
            for c in range(2):
                for t in tiles:
                    turn_back(t, 2 * h + c, turned[h][:, t, CHUNKS[c]])

        def look_up_both(h, t):
            fetch_scalar(fetched[h, t], t, HALVES[h])
            add_second(pairs[h, t], t, HALVES[h], fetched[h, t])

        for half in HALVES:
            square(0, half)
        fetch_vector(fetched["whole"], 0, 0, everyone)
        fetch_vector(pairs["whole"], 0, 1, everyone)
        square(1, everyone)
        fetch_vector(pairs[0, 1], 1, 1, first)
        square(2, everyone)
        fetch_scalar(fetched[0, 1], 1, first)
        square(last, everyone)
        look_up_both(0, 2)
        look_up_both(0, last)
        look_up_both(1, 1)
        fetched[1, last] = held.tile([P, S // 2], F32, name="fetched1_3", tag="fetched0_3", align_bytes=64)[:]
        fetch_vector(fetched[1, last], last, 0, later)
        fetch_vector(fetched[1, 2][:, CHUNKS[1]], 2, 0, CHUNKS[3])
        fetch_scalar(fetched[1, 2][:, CHUNKS[0]], 2, CHUNKS[2])
        add_second(pairs[1, 2], 2, later, fetched[1, 2])
        add_second(pairs[1, last], last, later, fetched[1, last])

        w2_grouped = held.tile([P, N * PACK], BF16, name="w2_grouped", align_bytes=64)
        for h in range(2):
            nc.gpsimd.tensor_scalar(
                w2_grouped[:, N * 2 * h : N * 2 * (h + 1)].rearrange("p (c j) -> p c j", j=PACK),
                w2_raw[h][:].rearrange("p j c -> p c j"),
                1.0,
                0.0,
                ALU.mult,
                ALU.add,
            )
        w2_codes = held.tile([P, N], U32, name="w2_codes", tag="fetched1_2", align_bytes=64)
        nc.vector.quantize_mx(out=w2_codes[:].bitcast(FP8X4), scales=w2_scales[:], in_=w2_grouped[:])

        for half in HALVES:
            gain_y(0, half)
        roots_of(0, (0, 1), "sums0")
        roots_of(0, (2,), "sums1")
        gain_y(1, first)
        gain_y(2, first)
        roots_of(0, (3,), "y0_0")
        gain_y(3, first)
        for tiles in ((0, 1), (2,), (3,)):
            roots_back(0, tiles)
        normalise(0)
        normalise(1)
        roots_of(1, (0, 1), "sums2")
        roots_of(1, (2,), "sums1")
        gain_y(1, later)
        roots_of(1, (3,), "y0_0")
        gain_y(2, later)
        gain_y(3, later)
        for tiles in ((0, 1), (2,), (3,)):
            roots_back(1, tiles)
        for piece in CHUNKS[:2]:
            quantise_z(piece)
        banks = out_banks(0, ("y0_0", "y3_0"))
        second_layer(first, banks, range(N // P))
        for b in range(len(banks)):
            store(0, banks, b, nc.scalar.copy)
        normalise(2)
        normalise(3)
        banks = out_banks(1, ("sums0", "y0_256", "y1_0", "y2_0"))
        for piece in CHUNKS[2:]:
            quantise_z(piece)
            second_layer(piece, banks, (0, 1))
        second_layer(later, banks, (2, 3))
        for b in range(len(banks)):
            store(1, banks, b, nc.vector.tensor_copy if b % 2 else nc.scalar.copy)
